import numpy as np
import ml_dtypes


def mxq(x, axis, fmt="e4m3"):
    dtype, down = {"e4m3": (ml_dtypes.float8_e4m3fn, 7), "e5m2": (ml_dtypes.float8_e5m2, 14)}[fmt]
    v = np.moveaxis(np.asarray(x, np.float32).astype(ml_dtypes.bfloat16).astype(np.float64), axis, -1)
    blocks = v.reshape(v.shape[:-1] + (-1, 32))
    amax = np.abs(blocks).max(-1, keepdims=True)
    byte = np.maximum(np.where(amax > 0, np.frexp(amax)[1] - 1 + 127, 0) - down, 1)
    scale = np.exp2(byte - 127.0)
    codes = (blocks / scale).astype(np.float32).astype(dtype).astype(np.float64)
    return np.moveaxis((codes * scale).reshape(v.shape), -1, axis)


WIDE = False


def mx_kscale(k):
    if not WIDE:
        return np.ones(k)
    levels = np.array([10, -10, 5, -5, 0])
    if k % 512:
        return np.exp2(np.random.permutation(np.resize(levels, k // 32))).repeat(32)
    a = np.empty((k // 512, 16))
    for p in range(k // 512):
        a[p, :8] = np.random.permutation(np.resize(levels, 8))
        for g in range(8):
            far = levels[np.abs(levels - a[p, g]) >= 10]
            a[p, g + 8] = far[np.random.randint(len(far))]
    return np.exp2(a.ravel()).repeat(32)


def f64(x):
    return np.asarray(x).astype(np.float64)


def striped(idx):
    return np.tile(np.asarray(idx).reshape(-1, 16).T, (8, 1)).astype(np.uint16)


def unstriped(offs):
    return offs[:16].T.reshape(-1).astype(np.int64)


E2M1 = np.array([0.0, 0.5, 1.0, 1.5, 2.0, 3.0, 4.0, 6.0, -0.0, -0.5, -1.0, -1.5, -2.0, -3.0, -4.0, -6.0])


def pack_weight(w, fmt):
    k, n = w.shape
    w = f64(np.asarray(w, np.float32).astype(ml_dtypes.bfloat16)).reshape(k // 32, 32, n)
    amax = np.abs(w).max(1)
    if fmt == "e4m3":
        byte = np.frexp(amax)[1] - 1 + 127 - 7
    else:
        mant, ex = np.frexp(amax / 6.0)
        byte = np.where(mant > 0.5, ex, ex - 1) + 127
    byte = np.clip(np.where(amax > 0, byte, 1), 1, 254)
    scaled = (w * np.exp2(127.0 - byte)[:, None, :]).reshape(k, n).astype(np.float32)
    by_word = np.ascontiguousarray(scaled.reshape(k // 512, 128, 4, n).transpose(0, 1, 3, 2))
    if fmt == "e4m3":
        words = by_word.astype(ml_dtypes.float8_e4m3fn).view(np.uint8)
    else:
        c = by_word.astype(ml_dtypes.float4_e2m1fn).view(np.uint8) & 0xF
        words = (c[..., 0::2] | (c[..., 1::2] << 4)).reshape(k // 512, 128, 2 * n)
    return np.ascontiguousarray(words), np.ascontiguousarray(byte.astype(np.uint8).reshape(k // 512, 16, n))


def unpack_weight(words, scales, fmt):
    g, _, n = scales.shape
    words = np.ascontiguousarray(words).reshape(g, 128, n, -1)
    if fmt == "e4m3":
        vals = words.view(ml_dtypes.float8_e4m3fn).astype(np.float64)
    else:
        nib = np.empty((g, 128, n, 4), np.uint8)
        nib[..., 0::2] = words & 0xF
        nib[..., 1::2] = words >> 4
        vals = E2M1[nib]
    vals = vals * np.repeat(np.exp2(scales.astype(np.float64) - 127.0), 8, axis=1)[..., None]
    return vals.transpose(0, 1, 3, 2).reshape(g * 512, n)


def bf(x):
    return np.asarray(x, np.float32).astype(ml_dtypes.bfloat16)


def planes(Y):
    r, m = Y.shape
    b = f64(bf(Y)).reshape(r // 32, 32, m)
    amax = np.abs(b).max(1)
    byte = np.clip(np.where(amax > 0, np.frexp(amax)[1] - 1 + 127 - 7, 1), 1, 254)
    codes = (b * np.exp2(127.0 - byte)[:, None, :]).reshape(r, m).astype(np.float32).astype(ml_dtypes.float8_e4m3fn).view(np.uint8)
    words = codes.reshape(r // 512, 128, 4, m).transpose(0, 1, 3, 2)
    return np.ascontiguousarray(words), np.ascontiguousarray(byte.astype(np.uint8).reshape(r // 512, 16, m))


D, T, I, Q, E = 512, 2048, 512, 256, 512


def setup_inputs():
    n = np.random.standard_normal
    idx = np.random.permutation(T)[:I]
    fd = mx_kscale(D)
    fi = mx_kscale(I)
    ti = np.ones(T)
    ti[idx] = fi
    keysp = pack_weight(n((D, T)) / fd[:, None], "e2m1")
    return {
        "query": (n((D, Q)) * 0.5 / np.sqrt(D) * fd[:, None]).astype(np.float32),
        "keys_words": keysp[0],
        "keys_scales": keysp[1],
        "fac": (np.random.uniform(0.5, 2.0, (I, 1)) * fi[:, None]).astype(np.float32),
        "vals": (n((E, T)) / ti).astype(np.float32),
        "offs": striped(idx),
    }


def reference(query, keys_words, keys_scales, fac, vals, offs):
    idx = unstriped(offs)
    keysu = unpack_weight(keys_words, keys_scales, "e2m1")
    keysidxg = keysu[:, idx]
    queryq = mxq(f64(query), 0, "e4m3")
    a = keysidxg.T @ queryq
    p = np.exp(a - np.max(a, axis=1, keepdims=True))
    w = p * f64(fac) / np.sum(p, axis=1, keepdims=True)
    vt = f64(vals)[:, idx].T
    vtq = mxq(vt, 0, "e4m3")
    wq = mxq(w, 0, "e4m3")
    o = vtq.T @ wq
    words, scales = planes(o)
    return o, words, scales

@@ -1,0 +1,213 @@
+from contextlib import ExitStack
+
+import concourse.mybir as mybir
+from concourse.masks import make_identity
+
+D, T, I, Q, E = 512, 2048, 512, 256, 512
+FLOPS = 2 * I * D * Q + 2 * E * I * Q
+
+F32 = mybir.dt.float32
+BF16 = mybir.dt.bfloat16
+I32 = mybir.dt.int32
+U32 = mybir.dt.uint32
+U16 = mybir.dt.uint16
+U8 = mybir.dt.uint8
+FP8X4 = mybir.dt.float8_e4m3fn_x4
+FP4X4 = mybir.dt.float4_e2m1fn_x4
+ACT = mybir.ActivationFunctionType
+ALU = mybir.AluOpType
+AXIS = mybir.AxisListType
+
+P = 128
+PACK = 4
+HALF_Q = Q // 2
+POOL_BYTES = T * 4
+
+
+def tile_attend_slotattn_pl_kernel(tc, query, keys_words, keys_scales, fac, vals, offs, out_0, out_1, out_2):
+    nc = tc.nc
+    with ExitStack() as ctx:
+        keep = ctx.enter_context(tc.tile_pool(name="keep", bufs=1))
+        reuse = ctx.enter_context(tc.tile_pool(name="reuse", bufs=1))
+        psum = ctx.enter_context(tc.psum_pool(name="psum", bufs=1))
+
+        def sb(shape, dtype, name):
+            return keep.tile(shape, dtype, name=name, align_bytes=64)
+
+        def over_pool(j, at, shape, dtype, name):
+            return reuse.tile(shape, dtype, name=name, align_bytes=64, offset=j * POOL_BYTES + at)
+
+        key_scales = sb([P, T], U8, "key_scales")
+        nc.gpsimd.memset(key_scales[:].bitcast(I32), 0)
+        offsets = keep.tile([P, I // 16], U16, name="offsets")
+        nc.sync.dma_start(offsets[:], offs)
+        for quad in range(4):
+            nc.sync.dma_start(
+                key_scales[32 * quad : 32 * quad + 4, :].bitcast(I32),
+                keys_scales[0, 4 * quad : 4 * quad + 4, :].bitcast(I32),
+            )
+        key_words = sb([P, T], U16, "key_words")
+        nc.sync.dma_start(key_words[:].bitcast(I32), keys_words[0].bitcast(I32))
+        query_rows = sb([P, PACK, Q], F32, "query_rows")
+        nc.sync.dma_start(query_rows[:], query.rearrange("(p j) q -> p j q", j=PACK))
+        fac_rows = sb([P, PACK], F32, "fac_rows")
+        nc.sync.dma_start(fac_rows[:], fac.rearrange("(p t) o -> p (t o)", t=PACK))
+        vals_rows = vals.rearrange("(p j) t -> j p t", j=PACK)
+        val_pool = []
+        for j in range(PACK):
+            tile = over_pool(j, 0, [P, T], F32, "val_pool%d" % j)
+            nc.sync.dma_start(tile[:], vals_rows[j])
+            val_pool.append(tile)
+
+        identity = sb([P, P], F32, "identity")
+        make_identity(nc, identity[:])
+        warm = sb([P, 1], F32, "warm")
+        nc.scalar.activation(out=warm[:], in_=identity[:, 0:1], func=ACT.Exp)
+
+        scales_listed = sb([P, I], U8, "scales_listed")
+        scales_dealt = sb([P, I], U8, "scales_dealt")
+        words_listed = sb([P, I], U16, "words_listed")
+        words_dealt = sb([P, I], U16, "words_dealt")
+        for window, listed in ((key_scales, scales_listed), (key_words, words_listed)):
+            nc.vector.tensor_copy(listed[:], window[:].indirect(offsets[:]))
+        for dealt, listed in ((scales_dealt, scales_listed), (words_dealt, words_listed)):
+            nc.vector.tensor_copy(
+                dealt[:].rearrange("p (t s) -> p t s", t=PACK),
+                listed[:].rearrange("p (s t) -> p t s", t=PACK),
+            )
+
+        query_bf = sb([P, Q, PACK], BF16, "query_bf")
+        nc.scalar.copy(
+            query_bf[:].rearrange("p (c i) j -> p c j i", i=4),
+            query_rows[:].rearrange("p j (c i) -> p c j i", i=4),
+        )
+        query_codes = sb([P, Q], U32, "query_codes")
+        query_scales = sb([P, Q], U8, "query_scales")
+        nc.vector.quantize_mx(
+            out=query_codes[:].bitcast(FP8X4), scales=query_scales[:], in_=query_bf[:].rearrange("p q j -> p (q j)")
+        )
+
+        scores = [psum.tile([P, 2, Q], F32, name="scores%d" % u) for u in range(2)]
+        for t in range(PACK):
+            cols = slice(t * P, (t + 1) * P)
+            nc.tensor.matmul_mx(
+                out=scores[t // 2][:, t % 2, :],
+                lhsT=words_dealt[:, cols].bitcast(FP4X4),
+                lhsT_scale=scales_dealt[:, cols],
+                rhs=query_codes[:].bitcast(FP8X4),
+                rhs_scale=query_scales[:],
+                start=True,
+                stop=True,
+            )
+
+        def gather_and_turn(j):
+            vals_listed = sb([P, I], BF16, "vals_listed%d" % j)
+            nc.vector.tensor_copy(vals_listed[:], val_pool[j][:].indirect(offsets[:]))
+            turned = psum.tile([P, 2, P], F32, name="turned%d" % j)
+            pairs = vals_listed[:].bitcast(F32)
+            for u in range(2):
+                nc.tensor.transpose(turned[:, u, :], pairs[:, u : 2 * P : 2], identity[:])
+            vals_bf = sb([P, P * PACK], BF16, "vals_bf%d" % j)
+            nc.scalar.copy(
+                vals_bf[:].bitcast(F32).rearrange("p (e u) -> p e u", u=2), turned[:].rearrange("p u e -> p e u")
+            )
+            return vals_bf
+
+        def quantise_vals(vals_bf, val_codes, j):
+            val_scales = sb([P, P], U8, "val_scales%d" % j)
+            nc.vector.quantize_mx(out=val_codes[:].bitcast(FP8X4), scales=val_scales[:], in_=vals_bf[:])
+            return val_codes, val_scales
+
+        probs = sb([P, PACK, Q], F32, "probs")
+        sums = sb([P, PACK], F32, "sums")
+        for u in range(2):
+            neg_max = sb([P, 2], F32, "neg_max%d" % u)
+            nc.vector.tensor_reduce(out=neg_max[:], in_=scores[u][:], axis=AXIS.X, op=ALU.max, negate=True)
+            for h in range(2):
+                t = 2 * u + h
+                nc.scalar.activation(
+                    out=probs[:, t, :], in_=scores[u][:, h, :], func=ACT.Exp,
+                    bias=neg_max[:, h : h + 1], scale=1.0, accum_out=sums[:, t : t + 1],
+                )
+
+        vals_bf0 = gather_and_turn(0)
+
+        inverse = over_pool(0, 0, [P, PACK], F32, "inverse")
+        nc.vector.reciprocal(inverse[:], sums[:])
+        share = sb([P, PACK], F32, "share")
+        nc.vector.tensor_tensor(share[:], inverse[:], fac_rows[:], ALU.mult)
+        weight_rows = sb([P, PACK, Q], BF16, "weight_rows")
+        for t in range(PACK):
+            nc.scalar.activation(
+                out=weight_rows[:, t, :], in_=probs[:, t, :], func=ACT.Copy, scale=share[:, t : t + 1]
+            )
+
+        vals_bf1 = gather_and_turn(1)
+        val_mx = [quantise_vals(vals_bf0, over_pool(1, 0, [P, P], U32, "val_codes0"), 0)]
+        vals_bf2 = gather_and_turn(2)
+
+        weight_bf = over_pool(2, 0, [P, Q, PACK], BF16, "weight_bf")
+        halves = [slice(half * HALF_Q, (half + 1) * HALF_Q) for half in range(2)]
+        for copy, cols in zip((nc.vector.tensor_copy, nc.scalar.copy), halves):
+            copy(
+                weight_bf[:, cols, :].rearrange("p (c i) t -> p c t i", i=4),
+                weight_rows[:, :, cols].rearrange("p t (c i) -> p c t i", i=4),
+            )
+        val_mx.append(quantise_vals(vals_bf1, over_pool(2, 4096, [P, P], U32, "val_codes1"), 1))
+        weight_codes = sb([P, Q], U32, "weight_codes")
+        weight_scales = sb([P, Q], U8, "weight_scales")
+        nc.vector.quantize_mx(
+            out=weight_codes[:].bitcast(FP8X4), scales=weight_scales[:], in_=weight_bf[:].rearrange("p q t -> p (q t)")
+        )
+        val_mx.append(quantise_vals(vals_bf2, sb([P, P], U32, "val_codes2"), 2))
+
+        sums_out = [psum.tile([P, PACK, HALF_Q], F32, name="sums_out%d" % half) for half in range(2)]
+        out_rows = out_0.rearrange("(p j) q -> p j q", j=PACK)
+
+        def multiply(j):
+            val_codes, val_scales = val_mx[j]
+            for half, cols in enumerate(halves):
+                nc.tensor.matmul_mx(
+                    out=sums_out[half][:, j, :],
+                    lhsT=val_codes[:].bitcast(FP8X4),
+                    lhsT_scale=val_scales[:],
+                    rhs=weight_codes[:, cols].bitcast(FP8X4),
+                    rhs_scale=weight_scales[:, cols],
+                    start=True,
+                    stop=True,
+                )
+
+        for j in range(PACK - 1):
+            multiply(j)
+        result_early = sb([P, PACK - 1, Q], F32, "result_early")
+        for half, cols in enumerate(halves):
+            nc.scalar.copy(result_early[:, :, cols], sums_out[half][:, : PACK - 1, :])
+        nc.sync.dma_start(out_rows[:, : PACK - 1, :], result_early[:])
+
+        vals_bf3 = gather_and_turn(3)
+        val_mx.append(quantise_vals(vals_bf3, sb([P, P], U32, "val_codes3"), 3))
+        multiply(PACK - 1)
+
+        result_bf = [sb([P, HALF_Q, PACK], BF16, "result_bf%d" % half) for half in range(2)]
+        nc.scalar.copy(result_bf[0][:], sums_out[0][:].rearrange("p j q -> p q j"))
+        nc.vector.tensor_copy(result_bf[1][:], sums_out[1][:].rearrange("p j q -> p q j"))
+        result_last = sb([P, Q], F32, "result_last")
+        for half, cols in enumerate(halves):
+            nc.scalar.copy(result_last[:, cols], sums_out[half][:, PACK - 1, :])
+        nc.sync.dma_start(out_rows[:, PACK - 1, :], result_last[:])
+
+        plane_codes = sb([P, Q], U32, "plane_codes")
+        plane_scales = sb([P, Q], U8, "plane_scales")
+        for half in range(2):
+            nc.vector.quantize_mx(
+                out=plane_codes[:, halves[half]].bitcast(FP8X4),
+                scales=plane_scales[:, halves[half]],
+                in_=result_bf[half][:].rearrange("p q j -> p (q j)"),
+            )
+        nc.sync.dma_start(out_1[0].rearrange("p c r -> p (c r)").bitcast(I32), plane_codes[:].bitcast(I32))
+        for quad in range(4):
+            engine = nc.scalar if quad % 2 else nc.sync
+            engine.dma_start(
+                out_2[0, 4 * quad : 4 * quad + 4, :].bitcast(I32),
+                plane_scales[32 * quad : 32 * quad + 4, :].bitcast(I32),
+            )

@@ -100,23 +100,28 @@ def tile_attend_slotattn_pl_kernel(tc, query, keys_words, keys_scales, fac, vals
                 stop=True,
             )
 
-        def gather_and_turn(j):
-            vals_listed = sb([P, I], BF16, "vals_listed%d" % j)
+        def gather_and_turn(j, vals_bf):
+            vals_listed = over_pool(PACK, j * 2 * I * 2, [P, I], BF16, "vals_listed%d" % j)
             nc.vector.tensor_copy(vals_listed[:], val_pool[j][:].indirect(offsets[:]))
-            turned = psum.tile([P, 2, P], F32, name="turned%d" % j)
+            turned = psum.tile([P, 2, P], F32, name="turned%d" % (j % 2))
             pairs = vals_listed[:].bitcast(F32)
             for u in range(2):
                 nc.tensor.transpose(turned[:, u, :], pairs[:, u : 2 * P : 2], identity[:])
-            vals_bf = sb([P, P * PACK], BF16, "vals_bf%d" % j)
             nc.scalar.copy(
-                vals_bf[:].bitcast(F32).rearrange("p (e u) -> p e u", u=2), turned[:].rearrange("p u e -> p e u")
+                vals_bf.bitcast(F32).rearrange("p (e u) -> p e u", u=2), turned[:].rearrange("p u e -> p e u")
             )
-            return vals_bf
 
-        def quantise_vals(vals_bf, val_codes, j):
-            val_scales = sb([P, P], U8, "val_scales%d" % j)
+        def quantise_vals(vals_bf, val_codes):
+            width = val_codes.shape[1]
+            val_scales = sb([P, width], U8, "val_scales%d" % len(val_mx))
             nc.vector.quantize_mx(out=val_codes[:].bitcast(FP8X4), scales=val_scales[:], in_=vals_bf[:])
-            return val_codes, val_scales
+            for start in range(0, width, P):
+                val_mx.append((val_codes[:, start : start + P], val_scales[:, start : start + P]))
+
+        val_mx = []
+        vals_bf01 = sb([P, 2 * I], BF16, "vals_bf01")
+        vals_bf2 = sb([P, I], BF16, "vals_bf2")
+        vals_bf3 = sb([P, I], BF16, "vals_bf3")
 
         probs = sb([P, PACK, Q], F32, "probs")
         sums = sb([P, PACK], F32, "sums")
@@ -130,74 +135,71 @@ def tile_attend_slotattn_pl_kernel(tc, query, keys_words, keys_scales, fac, vals
                     bias=neg_max[:, h : h + 1], scale=1.0, accum_out=sums[:, t : t + 1],
                 )
 
-        vals_bf0 = gather_and_turn(0)
+        gather_and_turn(0, vals_bf01[:, :I])
+        gather_and_turn(1, vals_bf01[:, I:])
 
-        inverse = over_pool(0, 0, [P, PACK], F32, "inverse")
+        inverse = over_pool(1, 0, [P, PACK], F32, "inverse")
         nc.vector.reciprocal(inverse[:], sums[:])
         share = sb([P, PACK], F32, "share")
         nc.vector.tensor_tensor(share[:], inverse[:], fac_rows[:], ALU.mult)
-        weight_rows = sb([P, PACK, Q], BF16, "weight_rows")
+        weight_rows = over_pool(PACK, 2 * I * 2, [P, PACK, Q], BF16, "weight_rows")
         for t in range(PACK):
             nc.scalar.activation(
                 out=weight_rows[:, t, :], in_=probs[:, t, :], func=ACT.Copy, scale=share[:, t : t + 1]
             )
 
-        vals_bf1 = gather_and_turn(1)
-        val_mx = [quantise_vals(vals_bf0, over_pool(1, 0, [P, P], U32, "val_codes0"), 0)]
-        vals_bf2 = gather_and_turn(2)
-
-        weight_bf = over_pool(2, 0, [P, Q, PACK], BF16, "weight_bf")
+        gather_and_turn(2, vals_bf2[:])
+        quantise_vals(vals_bf01, over_pool(2, 0, [P, 2 * P], U32, "val_codes01"))
         halves = [slice(half * HALF_Q, (half + 1) * HALF_Q) for half in range(2)]
-        for copy, cols in zip((nc.vector.tensor_copy, nc.scalar.copy), halves):
-            copy(
-                weight_bf[:, cols, :].rearrange("p (c i) t -> p c t i", i=4),
-                weight_rows[:, :, cols].rearrange("p t (c i) -> p c t i", i=4),
-            )
-        val_mx.append(quantise_vals(vals_bf1, over_pool(2, 4096, [P, P], U32, "val_codes1"), 1))
-        weight_codes = sb([P, Q], U32, "weight_codes")
+
+        def interleave(copy, out, rows):
+            copy(out.rearrange("p (c i) t -> p c t i", i=4), rows.rearrange("p t (c i) -> p c t i", i=4))
+
+        weight_bf = sb([P, Q, PACK], BF16, "weight_bf")
+        interleave(nc.scalar.copy, weight_bf[:], weight_rows[:])
+        gather_and_turn(3, vals_bf3[:])
+        weight_codes = over_pool(3, 0, [P, Q], U32, "weight_codes")
         weight_scales = sb([P, Q], U8, "weight_scales")
         nc.vector.quantize_mx(
             out=weight_codes[:].bitcast(FP8X4), scales=weight_scales[:], in_=weight_bf[:].rearrange("p q t -> p (q t)")
         )
-        val_mx.append(quantise_vals(vals_bf2, sb([P, P], U32, "val_codes2"), 2))
+        quantise_vals(vals_bf2, over_pool(3, 4096, [P, P], U32, "val_codes2"))
+        quantise_vals(vals_bf3, sb([P, P], U32, "val_codes3"))
 
-        sums_out = [psum.tile([P, PACK, HALF_Q], F32, name="sums_out%d" % half) for half in range(2)]
         out_rows = out_0.rearrange("(p j) q -> p j q", j=PACK)
+        result = sb([P, PACK, Q], F32, "result")
 
-        def multiply(j):
+        def multiply(out, j, cols):
             val_codes, val_scales = val_mx[j]
-            for half, cols in enumerate(halves):
-                nc.tensor.matmul_mx(
-                    out=sums_out[half][:, j, :],
-                    lhsT=val_codes[:].bitcast(FP8X4),
-                    lhsT_scale=val_scales[:],
-                    rhs=weight_codes[:, cols].bitcast(FP8X4),
-                    rhs_scale=weight_scales[:, cols],
-                    start=True,
-                    stop=True,
-                )
+            nc.tensor.matmul_mx(
+                out=out,
+                lhsT=val_codes.bitcast(FP8X4),
+                lhsT_scale=val_scales,
+                rhs=weight_codes[:, cols].bitcast(FP8X4),
+                rhs_scale=weight_scales[:, cols],
+                start=True,
+                stop=True,
+            )
 
-        for j in range(PACK - 1):
-            multiply(j)
-        result_early = sb([P, PACK - 1, Q], F32, "result_early")
-        for half, cols in enumerate(halves):
-            nc.scalar.copy(result_early[:, :, cols], sums_out[half][:, : PACK - 1, :])
-        nc.sync.dma_start(out_rows[:, : PACK - 1, :], result_early[:])
-
-        vals_bf3 = gather_and_turn(3)
-        val_mx.append(quantise_vals(vals_bf3, sb([P, P], U32, "val_codes3"), 3))
-        multiply(PACK - 1)
-
-        result_bf = [sb([P, HALF_Q, PACK], BF16, "result_bf%d" % half) for half in range(2)]
-        nc.scalar.copy(result_bf[0][:], sums_out[0][:].rearrange("p j q -> p q j"))
-        nc.vector.tensor_copy(result_bf[1][:], sums_out[1][:].rearrange("p j q -> p q j"))
-        result_last = sb([P, Q], F32, "result_last")
-        for half, cols in enumerate(halves):
-            nc.scalar.copy(result_last[:, cols], sums_out[half][:, PACK - 1, :])
-        nc.sync.dma_start(out_rows[:, PACK - 1, :], result_last[:])
+        sums01 = psum.tile([P, 2, Q], F32, name="sums01")
+        for j in range(2):
+            multiply(sums01[:, j, :], j, slice(0, Q))
+        nc.scalar.copy(result[:, :2, :], sums01[:])
+        sums2 = psum.tile([P, Q], F32, name="sums2")
+        multiply(sums2[:], 2, slice(0, Q))
+        nc.vector.tensor_copy(result[:, 2, :], sums2[:])
+        nc.sync.dma_start(out_rows[:, :3, :], result[:, :3, :])
+        for half, copy in enumerate((nc.vector.tensor_copy, nc.scalar.copy)):
+            sums3 = psum.tile([P, HALF_Q], F32, name="sums3_%d" % half)
+            multiply(sums3[:], 3, halves[half])
+            copy(result[:, 3, halves[half]], sums3[:])
+        nc.sync.dma_start(out_rows[:, 3, :], result[:, 3, :])
 
         plane_codes = sb([P, Q], U32, "plane_codes")
         plane_scales = sb([P, Q], U8, "plane_scales")
+        result_bf = [sb([P, HALF_Q, PACK], BF16, "result_bf%d" % half) for half in range(2)]
+        interleave(nc.vector.tensor_copy, result_bf[0][:], result[:, :, halves[0]])
+        interleave(nc.scalar.copy, result_bf[1][:], result[:, :, halves[1]])
         for half in range(2):
             nc.vector.quantize_mx(
                 out=plane_codes[:, halves[half]].bitcast(FP8X4),

@@ -41,11 +41,9 @@ def tile_attend_slotattn_pl_kernel(tc, query, keys_words, keys_scales, fac, vals
         nc.gpsimd.memset(key_scales[:].bitcast(I32), 0)
         offsets = keep.tile([P, I // 16], U16, name="offsets")
         nc.sync.dma_start(offsets[:], offs)
-        for quad in range(4):
-            nc.sync.dma_start(
-                key_scales[32 * quad : 32 * quad + 4, :].bitcast(I32),
-                keys_scales[0, 4 * quad : 4 * quad + 4, :].bitcast(I32),
-            )
+        scale_rows = keys_scales[0].rearrange("(quad r) t -> r quad t", r=4)
+        for r in range(4):
+            nc.sync.dma_start(key_scales[r:P:32, :].bitcast(I32), scale_rows[r].bitcast(I32))
         key_words = sb([P, T], U16, "key_words")
         nc.sync.dma_start(key_words[:].bitcast(I32), keys_words[0].bitcast(I32))
         query_rows = sb([P, PACK, Q], F32, "query_rows")
@@ -207,9 +205,7 @@ def tile_attend_slotattn_pl_kernel(tc, query, keys_words, keys_scales, fac, vals
                 in_=result_bf[half][:].rearrange("p q j -> p (q j)"),
             )
         nc.sync.dma_start(out_1[0].rearrange("p c r -> p (c r)").bitcast(I32), plane_codes[:].bitcast(I32))
-        for quad in range(4):
-            engine = nc.scalar if quad % 2 else nc.sync
-            engine.dma_start(
-                out_2[0, 4 * quad : 4 * quad + 4, :].bitcast(I32),
-                plane_scales[32 * quad : 32 * quad + 4, :].bitcast(I32),
-            )
+        out_scale_rows = out_2[0].rearrange("(quad r) q -> r quad q", r=4)
+        for r in range(4):
+            engine = nc.sync if r == 3 else nc.scalar
+            engine.dma_start(out_scale_rows[r].bitcast(I32), plane_scales[r:P:32, :].bitcast(I32))

@@ -59,8 +59,6 @@ def tile_attend_slotattn_pl_kernel(tc, query, keys_words, keys_scales, fac, vals
 
         identity = sb([P, P], F32, "identity")
         make_identity(nc, identity[:])
-        warm = sb([P, 1], F32, "warm")
-        nc.scalar.activation(out=warm[:], in_=identity[:, 0:1], func=ACT.Exp)
 
         scales_listed = sb([P, I], U8, "scales_listed")
         scales_dealt = sb([P, I], U8, "scales_dealt")
@@ -117,14 +115,13 @@ def tile_attend_slotattn_pl_kernel(tc, query, keys_words, keys_scales, fac, vals
                 val_mx.append((val_codes[:, start : start + P], val_scales[:, start : start + P]))
 
         val_mx = []
-        vals_bf01 = sb([P, 2 * I], BF16, "vals_bf01")
-        vals_bf2 = sb([P, I], BF16, "vals_bf2")
+        vals_bf12 = sb([P, 2 * I], BF16, "vals_bf12")
         vals_bf3 = sb([P, I], BF16, "vals_bf3")
 
         probs = sb([P, PACK, Q], F32, "probs")
         sums = sb([P, PACK], F32, "sums")
         for u in range(2):
-            neg_max = sb([P, 2], F32, "neg_max%d" % u)
+            neg_max = over_pool(PACK, 8192 + 4096 * u, [P, 2], F32, "neg_max%d" % u)
             nc.vector.tensor_reduce(out=neg_max[:], in_=scores[u][:], axis=AXIS.X, op=ALU.max, negate=True)
             for h in range(2):
                 t = 2 * u + h
@@ -133,11 +130,13 @@ def tile_attend_slotattn_pl_kernel(tc, query, keys_words, keys_scales, fac, vals
                     bias=neg_max[:, h : h + 1], scale=1.0, accum_out=sums[:, t : t + 1],
                 )
 
-        gather_and_turn(0, vals_bf01[:, :I])
-        gather_and_turn(1, vals_bf01[:, I:])
+        vals_bf0 = over_pool(PACK, 8192 + 4096, [P, I], BF16, "vals_bf0")
+        gather_and_turn(0, vals_bf0[:])
+        gather_and_turn(1, vals_bf12[:, :I])
 
-        inverse = over_pool(1, 0, [P, PACK], F32, "inverse")
+        inverse = sb([P, PACK], F32, "inverse")
         nc.vector.reciprocal(inverse[:], sums[:])
+        quantise_vals(vals_bf0, sb([P, P], U32, "val_codes0"))
         share = sb([P, PACK], F32, "share")
         nc.vector.tensor_tensor(share[:], inverse[:], fac_rows[:], ALU.mult)
         weight_rows = over_pool(PACK, 2 * I * 2, [P, PACK, Q], BF16, "weight_rows")
@@ -146,8 +145,7 @@ def tile_attend_slotattn_pl_kernel(tc, query, keys_words, keys_scales, fac, vals
                 out=weight_rows[:, t, :], in_=probs[:, t, :], func=ACT.Copy, scale=share[:, t : t + 1]
             )
 
-        gather_and_turn(2, vals_bf2[:])
-        quantise_vals(vals_bf01, over_pool(2, 0, [P, 2 * P], U32, "val_codes01"))
+        gather_and_turn(2, vals_bf12[:, I:])
         halves = [slice(half * HALF_Q, (half + 1) * HALF_Q) for half in range(2)]
 
         def interleave(copy, out, rows):
@@ -161,7 +159,7 @@ def tile_attend_slotattn_pl_kernel(tc, query, keys_words, keys_scales, fac, vals
         nc.vector.quantize_mx(
             out=weight_codes[:].bitcast(FP8X4), scales=weight_scales[:], in_=weight_bf[:].rearrange("p q t -> p (q t)")
         )
-        quantise_vals(vals_bf2, over_pool(3, 4096, [P, P], U32, "val_codes2"))
+        quantise_vals(vals_bf12, over_pool(3, 4096, [P, 2 * P], U32, "val_codes12"))
         quantise_vals(vals_bf3, sb([P, P], U32, "val_codes3"))
 
         out_rows = out_0.rearrange("(p j) q -> p j q", j=PACK)

@@ -21,6 +21,7 @@ AXIS = mybir.AxisListType
 P = 128
 PACK = 4
 HALF_Q = Q // 2
+SCALAR_Q = 64
 POOL_BYTES = T * 4
 
 
@@ -39,23 +40,24 @@ def tile_attend_slotattn_pl_kernel(tc, query, keys_words, keys_scales, fac, vals
 
         key_scales = sb([P, T], U8, "key_scales")
         nc.gpsimd.memset(key_scales[:].bitcast(I32), 0)
+        key_words = sb([P, T], U16, "key_words")
+        nc.sync.dma_start(key_words[:].bitcast(I32), keys_words[0].bitcast(I32))
         offsets = keep.tile([P, I // 16], U16, name="offsets")
         nc.sync.dma_start(offsets[:], offs)
         scale_rows = keys_scales[0].rearrange("(quad r) t -> r quad t", r=4)
         for r in range(4):
             nc.sync.dma_start(key_scales[r:P:32, :].bitcast(I32), scale_rows[r].bitcast(I32))
-        key_words = sb([P, T], U16, "key_words")
-        nc.sync.dma_start(key_words[:].bitcast(I32), keys_words[0].bitcast(I32))
         query_rows = sb([P, PACK, Q], F32, "query_rows")
         nc.sync.dma_start(query_rows[:], query.rearrange("(p j) q -> p j q", j=PACK))
         fac_rows = sb([P, PACK], F32, "fac_rows")
-        nc.sync.dma_start(fac_rows[:], fac.rearrange("(p t) o -> p (t o)", t=PACK))
         vals_rows = vals.rearrange("(p j) t -> j p t", j=PACK)
         val_pool = []
         for j in range(PACK):
             tile = over_pool(j, 0, [P, T], F32, "val_pool%d" % j)
             nc.sync.dma_start(tile[:], vals_rows[j])
             val_pool.append(tile)
+            if j == 0:
+                nc.sync.dma_start(fac_rows[:], fac.rearrange("(p t) o -> p (t o)", t=PACK))
 
         identity = sb([P, P], F32, "identity")
         make_identity(nc, identity[:])
@@ -72,7 +74,7 @@ def tile_attend_slotattn_pl_kernel(tc, query, keys_words, keys_scales, fac, vals
                 listed[:].rearrange("p (s t) -> p t s", t=PACK),
             )
 
-        query_bf = sb([P, Q, PACK], BF16, "query_bf")
+        query_bf = over_pool(PACK, 0, [P, Q, PACK], BF16, "query_bf")
         nc.scalar.copy(
             query_bf[:].rearrange("p (c i) j -> p c j i", i=4),
             query_rows[:].rearrange("p j (c i) -> p c j i", i=4),
@@ -115,7 +117,8 @@ def tile_attend_slotattn_pl_kernel(tc, query, keys_words, keys_scales, fac, vals
                 val_mx.append((val_codes[:, start : start + P], val_scales[:, start : start + P]))
 
         val_mx = []
-        vals_bf12 = sb([P, 2 * I], BF16, "vals_bf12")
+        vals_bf1 = sb([P, I], BF16, "vals_bf1")
+        vals_bf2 = sb([P, I], BF16, "vals_bf2")
         vals_bf3 = sb([P, I], BF16, "vals_bf3")
 
         probs = sb([P, PACK, Q], F32, "probs")
@@ -132,7 +135,7 @@ def tile_attend_slotattn_pl_kernel(tc, query, keys_words, keys_scales, fac, vals
 
         vals_bf0 = over_pool(PACK, 8192 + 4096, [P, I], BF16, "vals_bf0")
         gather_and_turn(0, vals_bf0[:])
-        gather_and_turn(1, vals_bf12[:, :I])
+        gather_and_turn(1, vals_bf1[:])
 
         inverse = sb([P, PACK], F32, "inverse")
         nc.vector.reciprocal(inverse[:], sums[:])
@@ -145,7 +148,8 @@ def tile_attend_slotattn_pl_kernel(tc, query, keys_words, keys_scales, fac, vals
                 out=weight_rows[:, t, :], in_=probs[:, t, :], func=ACT.Copy, scale=share[:, t : t + 1]
             )
 
-        gather_and_turn(2, vals_bf12[:, I:])
+        gather_and_turn(2, vals_bf2[:])
+        quantise_vals(vals_bf1, over_pool(2, 0, [P, P], U32, "val_codes1"))
         halves = [slice(half * HALF_Q, (half + 1) * HALF_Q) for half in range(2)]
 
         def interleave(copy, out, rows):
@@ -159,7 +163,7 @@ def tile_attend_slotattn_pl_kernel(tc, query, keys_words, keys_scales, fac, vals
         nc.vector.quantize_mx(
             out=weight_codes[:].bitcast(FP8X4), scales=weight_scales[:], in_=weight_bf[:].rearrange("p q t -> p (q t)")
         )
-        quantise_vals(vals_bf12, over_pool(3, 4096, [P, 2 * P], U32, "val_codes12"))
+        quantise_vals(vals_bf2, over_pool(3, 4096, [P, P], U32, "val_codes2"))
         quantise_vals(vals_bf3, sb([P, P], U32, "val_codes3"))
 
         out_rows = out_0.rearrange("(p j) q -> p j q", j=PACK)
@@ -177,15 +181,15 @@ def tile_attend_slotattn_pl_kernel(tc, query, keys_words, keys_scales, fac, vals
                 stop=True,
             )
 
-        sums01 = psum.tile([P, 2, Q], F32, name="sums01")
         for j in range(2):
-            multiply(sums01[:, j, :], j, slice(0, Q))
-        nc.scalar.copy(result[:, :2, :], sums01[:])
+            sums_j = psum.tile([P, Q], F32, name="scores%d" % j)
+            multiply(sums_j[:], j, slice(0, Q))
+            nc.scalar.copy(result[:, j, :], sums_j[:])
         sums2 = psum.tile([P, Q], F32, name="sums2")
         multiply(sums2[:], 2, slice(0, Q))
         nc.vector.tensor_copy(result[:, 2, :], sums2[:])
         nc.sync.dma_start(out_rows[:, :3, :], result[:, :3, :])
-        for half, copy in enumerate((nc.vector.tensor_copy, nc.scalar.copy)):
+        for half, copy in ((1, nc.scalar.copy), (0, nc.vector.tensor_copy)):
             sums3 = psum.tile([P, HALF_Q], F32, name="sums3_%d" % half)
             multiply(sums3[:], 3, halves[half])
             copy(result[:, 3, halves[half]], sums3[:])
@@ -194,9 +198,10 @@ def tile_attend_slotattn_pl_kernel(tc, query, keys_words, keys_scales, fac, vals
         plane_codes = sb([P, Q], U32, "plane_codes")
         plane_scales = sb([P, Q], U8, "plane_scales")
         result_bf = [sb([P, HALF_Q, PACK], BF16, "result_bf%d" % half) for half in range(2)]
-        interleave(nc.vector.tensor_copy, result_bf[0][:], result[:, :, halves[0]])
-        interleave(nc.scalar.copy, result_bf[1][:], result[:, :, halves[1]])
-        for half in range(2):
+        interleave(nc.vector.tensor_copy, result_bf[1][:], result[:, :, halves[1]])
+        interleave(nc.scalar.copy, result_bf[0][:, :SCALAR_Q, :], result[:, :, :SCALAR_Q])
+        interleave(nc.vector.tensor_copy, result_bf[0][:, SCALAR_Q:, :], result[:, :, SCALAR_Q:HALF_Q])
+        for half in (1, 0):
             nc.vector.quantize_mx(
                 out=plane_codes[:, halves[half]].bitcast(FP8X4),
                 scales=plane_scales[:, halves[half]],

@@ -38,52 +38,66 @@ def tile_attend_slotattn_pl_kernel(tc, query, keys_words, keys_scales, fac, vals
         def over_pool(j, at, shape, dtype, name):
             return reuse.tile(shape, dtype, name=name, align_bytes=64, offset=j * POOL_BYTES + at)
 
-        key_scales = sb([P, T], U8, "key_scales")
-        nc.gpsimd.memset(key_scales[:].bitcast(I32), 0)
-        key_words = sb([P, T], U16, "key_words")
-        nc.sync.dma_start(key_words[:].bitcast(I32), keys_words[0].bitcast(I32))
+        key_scales = over_pool(1, 0, [P, T], U8, "key_scales")
+        nc.vector.memset(key_scales[:].bitcast(I32), 0)
         offsets = keep.tile([P, I // 16], U16, name="offsets")
         nc.sync.dma_start(offsets[:], offs)
-        scale_rows = keys_scales[0].rearrange("(quad r) t -> r quad t", r=4)
-        for r in range(4):
-            nc.sync.dma_start(key_scales[r:P:32, :].bitcast(I32), scale_rows[r].bitcast(I32))
-        query_rows = sb([P, PACK, Q], F32, "query_rows")
-        nc.sync.dma_start(query_rows[:], query.rearrange("(p j) q -> p j q", j=PACK))
+        query_rows = [sb([P, 2, Q], F32, "query_rows%d" % u) for u in range(2)]
+        query_pairs = query.rearrange("(p u j) q -> u p j q", u=2, j=2)
+        nc.sync.dma_start(query_rows[0][:], query_pairs[0])
+        nc.sync.dma_start(key_scales[4:P:8, :].bitcast(I32), keys_scales[0].bitcast(I32))
+        key_words = over_pool(2, 0, [P, T], U16, "key_words")
+        nc.sync.dma_start(key_words[:].bitcast(I32), keys_words[0].bitcast(I32))
+        nc.sync.dma_start(query_rows[1][:], query_pairs[1])
         fac_rows = sb([P, PACK], F32, "fac_rows")
         vals_rows = vals.rearrange("(p j) t -> j p t", j=PACK)
         val_pool = []
-        for j in range(PACK):
+
+        def load_vals(j):
             tile = over_pool(j, 0, [P, T], F32, "val_pool%d" % j)
             nc.sync.dma_start(tile[:], vals_rows[j])
             val_pool.append(tile)
-            if j == 0:
-                nc.sync.dma_start(fac_rows[:], fac.rearrange("(p t) o -> p (t o)", t=PACK))
+
+        load_vals(0)
+        nc.sync.dma_start(fac_rows[:], fac.rearrange("(p t) o -> p (t o)", t=PACK))
 
         identity = sb([P, P], F32, "identity")
         make_identity(nc, identity[:])
 
         scales_listed = sb([P, I], U8, "scales_listed")
+        scales_moved = over_pool(PACK, 0, [P, I], U8, "scales_moved")
+        nc.gpsimd.memset(scales_moved[:].bitcast(I32), 0)
         scales_dealt = sb([P, I], U8, "scales_dealt")
-        words_listed = sb([P, I], U16, "words_listed")
+        words_listed = over_pool(3, 0, [P, I], U16, "words_listed")
         words_dealt = sb([P, I], U16, "words_dealt")
-        for window, listed in ((key_scales, scales_listed), (key_words, words_listed)):
-            nc.vector.tensor_copy(listed[:], window[:].indirect(offsets[:]))
-        for dealt, listed in ((scales_dealt, scales_listed), (words_dealt, words_listed)):
+
+        def deal(dealt, listed):
             nc.vector.tensor_copy(
                 dealt[:].rearrange("p (t s) -> p t s", t=PACK),
                 listed[:].rearrange("p (s t) -> p t s", t=PACK),
             )
 
-        query_bf = over_pool(PACK, 0, [P, Q, PACK], BF16, "query_bf")
-        nc.scalar.copy(
-            query_bf[:].rearrange("p (c i) j -> p c j i", i=4),
-            query_rows[:].rearrange("p j (c i) -> p c j i", i=4),
-        )
+        nc.vector.tensor_copy(scales_listed[:], key_scales[:].indirect(offsets[:]))
+        for r in range(4):
+            nc.sync.dma_start(scales_moved[r:P:32, :].bitcast(I32), scales_listed[8 * r + 4 : P : 32, :].bitcast(I32))
+        nc.vector.tensor_copy(words_listed[:], key_words[:].indirect(offsets[:]))
+        deal(words_dealt, words_listed)
+        for j in range(1, PACK):
+            load_vals(j)
+
+        query_bf = sb([P, Q, PACK], BF16, "query_bf")
+        for u in range(2):
+            nc.scalar.copy(
+                query_bf[:, :, 2 * u : 2 * u + 2].rearrange("p (c i) j -> p c j i", i=4),
+                query_rows[u][:].rearrange("p j (c i) -> p c j i", i=4),
+            )
         query_codes = sb([P, Q], U32, "query_codes")
         query_scales = sb([P, Q], U8, "query_scales")
         nc.vector.quantize_mx(
             out=query_codes[:].bitcast(FP8X4), scales=query_scales[:], in_=query_bf[:].rearrange("p q j -> p (q j)")
         )
+
+        deal(scales_dealt, scales_moved)
 
         scores = [psum.tile([P, 2, Q], F32, name="scores%d" % u) for u in range(2)]
         for t in range(PACK):
@@ -117,8 +131,7 @@ def tile_attend_slotattn_pl_kernel(tc, query, keys_words, keys_scales, fac, vals
                 val_mx.append((val_codes[:, start : start + P], val_scales[:, start : start + P]))
 
         val_mx = []
-        vals_bf1 = sb([P, I], BF16, "vals_bf1")
-        vals_bf2 = sb([P, I], BF16, "vals_bf2")
+        vals_bf12 = sb([P, 2 * I], BF16, "vals_bf12")
         vals_bf3 = sb([P, I], BF16, "vals_bf3")
 
         probs = sb([P, PACK, Q], F32, "probs")
@@ -135,7 +148,7 @@ def tile_attend_slotattn_pl_kernel(tc, query, keys_words, keys_scales, fac, vals
 
         vals_bf0 = over_pool(PACK, 8192 + 4096, [P, I], BF16, "vals_bf0")
         gather_and_turn(0, vals_bf0[:])
-        gather_and_turn(1, vals_bf1[:])
+        gather_and_turn(1, vals_bf12[:, :I])
 
         inverse = sb([P, PACK], F32, "inverse")
         nc.vector.reciprocal(inverse[:], sums[:])
@@ -148,8 +161,7 @@ def tile_attend_slotattn_pl_kernel(tc, query, keys_words, keys_scales, fac, vals
                 out=weight_rows[:, t, :], in_=probs[:, t, :], func=ACT.Copy, scale=share[:, t : t + 1]
             )
 
-        gather_and_turn(2, vals_bf2[:])
-        quantise_vals(vals_bf1, over_pool(2, 0, [P, P], U32, "val_codes1"))
+        gather_and_turn(2, vals_bf12[:, I:])
         halves = [slice(half * HALF_Q, (half + 1) * HALF_Q) for half in range(2)]
 
         def interleave(copy, out, rows):
@@ -163,7 +175,7 @@ def tile_attend_slotattn_pl_kernel(tc, query, keys_words, keys_scales, fac, vals
         nc.vector.quantize_mx(
             out=weight_codes[:].bitcast(FP8X4), scales=weight_scales[:], in_=weight_bf[:].rearrange("p q t -> p (q t)")
         )
-        quantise_vals(vals_bf2, over_pool(3, 4096, [P, P], U32, "val_codes2"))
+        quantise_vals(vals_bf12, over_pool(3, 4096, [P, 2 * P], U32, "val_codes12"))
         quantise_vals(vals_bf3, sb([P, P], U32, "val_codes3"))
 
         out_rows = out_0.rearrange("(p j) q -> p j q", j=PACK)

@@ -23,6 +23,8 @@ PACK = 4
 HALF_Q = Q // 2
 SCALAR_Q = 64
 POOL_BYTES = T * 4
+FIRST_ROW = 11
+ROW_STEP = 7
 
 
 def tile_attend_slotattn_pl_kernel(tc, query, keys_words, keys_scales, fac, vals, offs, out_0, out_1, out_2):
@@ -45,7 +47,7 @@ def tile_attend_slotattn_pl_kernel(tc, query, keys_words, keys_scales, fac, vals
         query_rows = [sb([P, 2, Q], F32, "query_rows%d" % u) for u in range(2)]
         query_pairs = query.rearrange("(p u j) q -> u p j q", u=2, j=2)
         nc.sync.dma_start(query_rows[0][:], query_pairs[0])
-        nc.sync.dma_start(key_scales[4:P:8, :].bitcast(I32), keys_scales[0].bitcast(I32))
+        nc.sync.dma_start(key_scales[FIRST_ROW : FIRST_ROW + 16 * ROW_STEP : ROW_STEP, :].bitcast(I32), keys_scales[0].bitcast(I32))
         key_words = over_pool(2, 0, [P, T], U16, "key_words")
         nc.sync.dma_start(key_words[:].bitcast(I32), keys_words[0].bitcast(I32))
         nc.sync.dma_start(query_rows[1][:], query_pairs[1])
@@ -64,8 +66,8 @@ def tile_attend_slotattn_pl_kernel(tc, query, keys_words, keys_scales, fac, vals
         identity = sb([P, P], F32, "identity")
         make_identity(nc, identity[:])
 
-        scales_listed = sb([P, I], U8, "scales_listed")
-        scales_moved = over_pool(PACK, 0, [P, I], U8, "scales_moved")
+        scales_listed = over_pool(PACK, 0, [P, I], U8, "scales_listed")
+        scales_moved = sb([P, I], U8, "scales_moved")
         nc.gpsimd.memset(scales_moved[:].bitcast(I32), 0)
         scales_dealt = sb([P, I], U8, "scales_dealt")
         words_listed = over_pool(3, 0, [P, I], U16, "words_listed")
@@ -79,7 +81,9 @@ def tile_attend_slotattn_pl_kernel(tc, query, keys_words, keys_scales, fac, vals
 
         nc.vector.tensor_copy(scales_listed[:], key_scales[:].indirect(offsets[:]))
         for r in range(4):
-            nc.sync.dma_start(scales_moved[r:P:32, :].bitcast(I32), scales_listed[8 * r + 4 : P : 32, :].bitcast(I32))
+            first = FIRST_ROW + r * ROW_STEP
+            rows = scales_listed[first : first + 13 * ROW_STEP : 4 * ROW_STEP, :]
+            nc.sync.dma_start(scales_moved[r:P:32, :].bitcast(I32), rows.bitcast(I32))
         nc.vector.tensor_copy(words_listed[:], key_words[:].indirect(offsets[:]))
         deal(words_dealt, words_listed)
         for j in range(1, PACK):

@@ -23,8 +23,8 @@ PACK = 4
 HALF_Q = Q // 2
 SCALAR_Q = 64
 POOL_BYTES = T * 4
-FIRST_ROW = 11
-ROW_STEP = 7
+FIRST_ROW = 32
+ROW_STEP = 4
 
 
 def tile_attend_slotattn_pl_kernel(tc, query, keys_words, keys_scales, fac, vals, offs, out_0, out_1, out_2):
@@ -64,11 +64,12 @@ def tile_attend_slotattn_pl_kernel(tc, query, keys_words, keys_scales, fac, vals
         nc.sync.dma_start(fac_rows[:], fac.rearrange("(p t) o -> p (t o)", t=PACK))
 
         identity = sb([P, P], F32, "identity")
-        make_identity(nc, identity[:])
+        nc.vector.memset(identity[:], 0.0)
+        make_identity(nc, identity[:], nomemset=True)
 
         scales_listed = over_pool(PACK, 0, [P, I], U8, "scales_listed")
         scales_moved = sb([P, I], U8, "scales_moved")
-        nc.gpsimd.memset(scales_moved[:].bitcast(I32), 0)
+        nc.vector.memset(scales_moved[:].bitcast(I32), 0)
         scales_dealt = sb([P, I], U8, "scales_dealt")
         words_listed = over_pool(3, 0, [P, I], U16, "words_listed")
         words_dealt = sb([P, I], U16, "words_dealt")
@@ -135,7 +136,8 @@ def tile_attend_slotattn_pl_kernel(tc, query, keys_words, keys_scales, fac, vals
                 val_mx.append((val_codes[:, start : start + P], val_scales[:, start : start + P]))
 
         val_mx = []
-        vals_bf12 = sb([P, 2 * I], BF16, "vals_bf12")
+        vals_bf1 = sb([P, I], BF16, "vals_bf1")
+        vals_bf2 = sb([P, I], BF16, "vals_bf2")
         vals_bf3 = sb([P, I], BF16, "vals_bf3")
 
         probs = sb([P, PACK, Q], F32, "probs")
@@ -152,7 +154,7 @@ def tile_attend_slotattn_pl_kernel(tc, query, keys_words, keys_scales, fac, vals
 
         vals_bf0 = over_pool(PACK, 8192 + 4096, [P, I], BF16, "vals_bf0")
         gather_and_turn(0, vals_bf0[:])
-        gather_and_turn(1, vals_bf12[:, :I])
+        gather_and_turn(1, vals_bf1[:])
 
         inverse = sb([P, PACK], F32, "inverse")
         nc.vector.reciprocal(inverse[:], sums[:])
@@ -165,7 +167,7 @@ def tile_attend_slotattn_pl_kernel(tc, query, keys_words, keys_scales, fac, vals
                 out=weight_rows[:, t, :], in_=probs[:, t, :], func=ACT.Copy, scale=share[:, t : t + 1]
             )
 
-        gather_and_turn(2, vals_bf12[:, I:])
+        gather_and_turn(2, vals_bf2[:])
         halves = [slice(half * HALF_Q, (half + 1) * HALF_Q) for half in range(2)]
 
         def interleave(copy, out, rows):
@@ -179,7 +181,8 @@ def tile_attend_slotattn_pl_kernel(tc, query, keys_words, keys_scales, fac, vals
         nc.vector.quantize_mx(
             out=weight_codes[:].bitcast(FP8X4), scales=weight_scales[:], in_=weight_bf[:].rearrange("p q t -> p (q t)")
         )
-        quantise_vals(vals_bf12, over_pool(3, 4096, [P, 2 * P], U32, "val_codes12"))
+        quantise_vals(vals_bf1, over_pool(3, 4096, [P, P], U32, "val_codes1"))
+        quantise_vals(vals_bf2, over_pool(3, 6144, [P, P], U32, "val_codes2"))
         quantise_vals(vals_bf3, sb([P, P], U32, "val_codes3"))
 
         out_rows = out_0.rearrange("(p j) q -> p j q", j=PACK)

@@ -25,6 +25,7 @@ SCALAR_Q = 64
 POOL_BYTES = T * 4
 FIRST_ROW = 32
 ROW_STEP = 4
+LAST_VECTOR = 256
 
 
 def tile_attend_slotattn_pl_kernel(tc, query, keys_words, keys_scales, fac, vals, offs, out_0, out_1, out_2):
@@ -68,9 +69,8 @@ def tile_attend_slotattn_pl_kernel(tc, query, keys_words, keys_scales, fac, vals
         make_identity(nc, identity[:], nomemset=True)
 
         scales_listed = over_pool(PACK, 0, [P, I], U8, "scales_listed")
-        scales_moved = sb([P, I], U8, "scales_moved")
-        nc.vector.memset(scales_moved[:].bitcast(I32), 0)
         scales_dealt = sb([P, I], U8, "scales_dealt")
+        nc.vector.memset(scales_dealt[:].bitcast(I32), 0)
         words_listed = over_pool(3, 0, [P, I], U16, "words_listed")
         words_dealt = sb([P, I], U16, "words_dealt")
 
@@ -80,11 +80,13 @@ def tile_attend_slotattn_pl_kernel(tc, query, keys_words, keys_scales, fac, vals
                 listed[:].rearrange("p (s t) -> p t s", t=PACK),
             )
 
-        nc.vector.tensor_copy(scales_listed[:], key_scales[:].indirect(offsets[:]))
+        nc.vector.tensor_copy(
+            scales_listed[:].rearrange("p (t s) -> p s t", t=PACK), key_scales[:].indirect(offsets[:])
+        )
         for r in range(4):
             first = FIRST_ROW + r * ROW_STEP
             rows = scales_listed[first : first + 13 * ROW_STEP : 4 * ROW_STEP, :]
-            nc.sync.dma_start(scales_moved[r:P:32, :].bitcast(I32), rows.bitcast(I32))
+            nc.sync.dma_start(scales_dealt[r:P:32, :].bitcast(I32), rows.bitcast(I32))
         nc.vector.tensor_copy(words_listed[:], key_words[:].indirect(offsets[:]))
         deal(words_dealt, words_listed)
         for j in range(1, PACK):
@@ -102,13 +104,11 @@ def tile_attend_slotattn_pl_kernel(tc, query, keys_words, keys_scales, fac, vals
             out=query_codes[:].bitcast(FP8X4), scales=query_scales[:], in_=query_bf[:].rearrange("p q j -> p (q j)")
         )
 
-        deal(scales_dealt, scales_moved)
-
-        scores = [psum.tile([P, 2, Q], F32, name="scores%d" % u) for u in range(2)]
+        scores = [psum.tile([P, Q], F32, name="scores%d" % t) for t in range(PACK)]
         for t in range(PACK):
             cols = slice(t * P, (t + 1) * P)
             nc.tensor.matmul_mx(
-                out=scores[t // 2][:, t % 2, :],
+                out=scores[t][:],
                 lhsT=words_dealt[:, cols].bitcast(FP4X4),
                 lhsT_scale=scales_dealt[:, cols],
                 rhs=query_codes[:].bitcast(FP8X4),
@@ -117,102 +117,106 @@ def tile_attend_slotattn_pl_kernel(tc, query, keys_words, keys_scales, fac, vals
                 stop=True,
             )
 
-        def gather_and_turn(j, vals_bf):
-            vals_listed = over_pool(PACK, j * 2 * I * 2, [P, I], BF16, "vals_listed%d" % j)
-            nc.vector.tensor_copy(vals_listed[:], val_pool[j][:].indirect(offsets[:]))
-            turned = psum.tile([P, 2, P], F32, name="turned%d" % (j % 2))
+        copy_act = lambda out, in_: nc.scalar.activation(out=out, in_=in_, func=ACT.Copy)
+
+        def gather(j, vals_listed, pieces):
+            for copy, first, last in pieces:
+                copy(vals_listed[:, first:last], val_pool[j][:].indirect(offsets[:, first // 16 : last // 16]))
+
+        def turn(vals_listed, bank, copy, vals_bf):
+            turned = psum.tile([P, 2, P], F32, name=bank)
             pairs = vals_listed[:].bitcast(F32)
             for u in range(2):
                 nc.tensor.transpose(turned[:, u, :], pairs[:, u : 2 * P : 2], identity[:])
-            nc.scalar.copy(
-                vals_bf.bitcast(F32).rearrange("p (e u) -> p e u", u=2), turned[:].rearrange("p u e -> p e u")
-            )
+            copy(vals_bf[:].bitcast(F32).rearrange("p (e u) -> p e u", u=2), turned[:].rearrange("p u e -> p e u"))
 
         def quantise_vals(vals_bf, val_codes):
-            width = val_codes.shape[1]
-            val_scales = sb([P, width], U8, "val_scales%d" % len(val_mx))
+            val_scales = sb([P, P], U8, "val_scales%d" % len(val_mx))
             nc.vector.quantize_mx(out=val_codes[:].bitcast(FP8X4), scales=val_scales[:], in_=vals_bf[:])
-            for start in range(0, width, P):
-                val_mx.append((val_codes[:, start : start + P], val_scales[:, start : start + P]))
+            val_mx.append((val_codes, val_scales))
 
         val_mx = []
-        vals_bf1 = sb([P, I], BF16, "vals_bf1")
-        vals_bf2 = sb([P, I], BF16, "vals_bf2")
-        vals_bf3 = sb([P, I], BF16, "vals_bf3")
+        vals_bf = [sb([P, I], BF16, "vals_bf%d" % j) for j in range(2)]
+        vals_listed0 = sb([P, I], BF16, "vals_listed0")
+        gather(0, vals_listed0, [(copy_act, 0, I)])
 
         probs = sb([P, PACK, Q], F32, "probs")
         sums = sb([P, PACK], F32, "sums")
-        for u in range(2):
-            neg_max = over_pool(PACK, 8192 + 4096 * u, [P, 2], F32, "neg_max%d" % u)
-            nc.vector.tensor_reduce(out=neg_max[:], in_=scores[u][:], axis=AXIS.X, op=ALU.max, negate=True)
-            for h in range(2):
-                t = 2 * u + h
-                nc.scalar.activation(
-                    out=probs[:, t, :], in_=scores[u][:, h, :], func=ACT.Exp,
-                    bias=neg_max[:, h : h + 1], scale=1.0, accum_out=sums[:, t : t + 1],
-                )
+        for t in range(PACK):
+            neg_max = over_pool(PACK, 8192 + 1024 * t, [P, 1], F32, "neg_max%d" % t)
+            nc.vector.tensor_reduce(out=neg_max[:], in_=scores[t][:], axis=AXIS.X, op=ALU.max, negate=True)
+            nc.scalar.activation(
+                out=probs[:, t, :], in_=scores[t][:], func=ACT.Exp,
+                bias=neg_max[:], scale=1.0, accum_out=sums[:, t : t + 1],
+            )
 
-        vals_bf0 = over_pool(PACK, 8192 + 4096, [P, I], BF16, "vals_bf0")
-        gather_and_turn(0, vals_bf0[:])
-        gather_and_turn(1, vals_bf1[:])
+        turn(vals_listed0, "scores0", nc.vector.tensor_copy, vals_bf[0])
+        vals_listed1 = over_pool(PACK, 8192 + 2048, [P, I], BF16, "vals_listed1")
+        gather(1, vals_listed1, [(copy_act, 0, I)])
 
         inverse = sb([P, PACK], F32, "inverse")
         nc.vector.reciprocal(inverse[:], sums[:])
-        quantise_vals(vals_bf0, sb([P, P], U32, "val_codes0"))
+        quantise_vals(vals_bf[0], sb([P, P], U32, "val_codes0"))
         share = sb([P, PACK], F32, "share")
         nc.vector.tensor_tensor(share[:], inverse[:], fac_rows[:], ALU.mult)
-        weight_rows = over_pool(PACK, 2 * I * 2, [P, PACK, Q], BF16, "weight_rows")
-        for t in range(PACK):
-            nc.scalar.activation(
-                out=weight_rows[:, t, :], in_=probs[:, t, :], func=ACT.Copy, scale=share[:, t : t + 1]
-            )
+        weight_bf = sb([P, Q, PACK], BF16, "weight_bf")
+        nc.vector.tensor_tensor(
+            weight_bf[:].rearrange("p (c i) t -> p c t i", i=4),
+            probs[:].rearrange("p t (c i) -> p c t i", i=4),
+            share[:].unsqueeze(1).unsqueeze(3).to_broadcast([P, Q // 4, PACK, 4]),
+            ALU.mult,
+        )
+        turn(vals_listed1, "scores1", nc.vector.tensor_copy, vals_bf[1])
+        weight_codes = sb([P, Q], U32, "weight_codes")
+        weight_scales = sb([P, Q], U8, "weight_scales")
+        nc.vector.quantize_mx(
+            out=weight_codes[:].bitcast(FP8X4), scales=weight_scales[:], in_=weight_bf[:].rearrange("p q t -> p (q t)")
+        )
+        quantise_vals(vals_bf[1], sb([P, P], U32, "val_codes1"))
 
-        gather_and_turn(2, vals_bf2[:])
+        vals_listed2 = sb([P, I], BF16, "vals_listed2")
+        gather(2, vals_listed2, [(copy_act, 0, I)])
         halves = [slice(half * HALF_Q, (half + 1) * HALF_Q) for half in range(2)]
 
         def interleave(copy, out, rows):
             copy(out.rearrange("p (c i) t -> p c t i", i=4), rows.rearrange("p t (c i) -> p c t i", i=4))
 
-        weight_bf = sb([P, Q, PACK], BF16, "weight_bf")
-        interleave(nc.scalar.copy, weight_bf[:], weight_rows[:])
-        gather_and_turn(3, vals_bf3[:])
-        weight_codes = over_pool(3, 0, [P, Q], U32, "weight_codes")
-        weight_scales = sb([P, Q], U8, "weight_scales")
-        nc.vector.quantize_mx(
-            out=weight_codes[:].bitcast(FP8X4), scales=weight_scales[:], in_=weight_bf[:].rearrange("p q t -> p (q t)")
-        )
-        quantise_vals(vals_bf1, over_pool(3, 4096, [P, P], U32, "val_codes1"))
-        quantise_vals(vals_bf2, over_pool(3, 6144, [P, P], U32, "val_codes2"))
-        quantise_vals(vals_bf3, sb([P, P], U32, "val_codes3"))
-
         out_rows = out_0.rearrange("(p j) q -> p j q", j=PACK)
-        result = sb([P, PACK, Q], F32, "result")
 
         def multiply(out, j, cols):
             val_codes, val_scales = val_mx[j]
             nc.tensor.matmul_mx(
                 out=out,
-                lhsT=val_codes.bitcast(FP8X4),
-                lhsT_scale=val_scales,
+                lhsT=val_codes[:].bitcast(FP8X4),
+                lhsT_scale=val_scales[:],
                 rhs=weight_codes[:, cols].bitcast(FP8X4),
                 rhs_scale=weight_scales[:, cols],
                 start=True,
                 stop=True,
             )
 
+        vals_listed3 = sb([P, I], BF16, "vals_listed3")
+        gather(3, vals_listed3, [(nc.vector.tensor_copy, 0, LAST_VECTOR), (copy_act, LAST_VECTOR, I)])
+        result = over_pool(3, 0, [P, PACK, Q], F32, "result")
+        products = [psum.tile([P, Q], F32, name="sums%d" % j) for j in range(2)]
         for j in range(2):
-            sums_j = psum.tile([P, Q], F32, name="scores%d" % j)
-            multiply(sums_j[:], j, slice(0, Q))
-            nc.scalar.copy(result[:, j, :], sums_j[:])
-        sums2 = psum.tile([P, Q], F32, name="sums2")
-        multiply(sums2[:], 2, slice(0, Q))
-        nc.vector.tensor_copy(result[:, 2, :], sums2[:])
-        nc.sync.dma_start(out_rows[:, :3, :], result[:, :3, :])
+            multiply(products[j][:], j, slice(0, Q))
+        nc.scalar.copy(result[:, 0, :], products[0][:])
+        vals_bf2 = over_pool(3, 4096, [P, I], BF16, "vals_bf2")
+        turn(vals_listed2, "scores2", nc.vector.tensor_copy, vals_bf2)
+        nc.vector.tensor_copy(result[:, 1, :], products[1][:])
+        nc.sync.dma_start(out_rows[:, :2, :], result[:, :2, :])
+        vals_bf3 = sb([P, I], BF16, "vals_bf3")
+        turn(vals_listed3, "scores3", nc.scalar.copy, vals_bf3)
+        quantise_vals(vals_bf2, sb([P, P], U32, "val_codes2"))
+        quantise_vals(vals_bf3, sb([P, P], U32, "val_codes3"))
+        sums23 = [psum.tile([P, 2, HALF_Q], F32, name="sums23_%d" % half) for half in range(2)]
+        for j in (2, 3):
+            for half in (1, 0):
+                multiply(sums23[half][:, j - 2, :], j, halves[half])
         for half, copy in ((1, nc.scalar.copy), (0, nc.vector.tensor_copy)):
-            sums3 = psum.tile([P, HALF_Q], F32, name="sums3_%d" % half)
-            multiply(sums3[:], 3, halves[half])
-            copy(result[:, 3, halves[half]], sums3[:])
-        nc.sync.dma_start(out_rows[:, 3, :], result[:, 3, :])
+            copy(result[:, 2:, halves[half]], sums23[half][:])
+        nc.sync.dma_start(out_rows[:, 2:, :], result[:, 2:, :])
 
         plane_codes = sb([P, Q], U32, "plane_codes")
         plane_scales = sb([P, Q], U8, "plane_scales")

@@ -44,10 +44,10 @@ def tile_attend_slotattn_pl_kernel(tc, query, keys_words, keys_scales, fac, vals
         key_scales = over_pool(1, 0, [P, T], U8, "key_scales")
         nc.vector.memset(key_scales[:].bitcast(I32), 0)
         offsets = keep.tile([P, I // 16], U16, name="offsets")
-        nc.sync.dma_start(offsets[:], offs)
         query_rows = [sb([P, 2, Q], F32, "query_rows%d" % u) for u in range(2)]
         query_pairs = query.rearrange("(p u j) q -> u p j q", u=2, j=2)
         nc.sync.dma_start(query_rows[0][:], query_pairs[0])
+        nc.sync.dma_start(offsets[:], offs)
         nc.sync.dma_start(key_scales[FIRST_ROW : FIRST_ROW + 16 * ROW_STEP : ROW_STEP, :].bitcast(I32), keys_scales[0].bitcast(I32))
         key_words = over_pool(2, 0, [P, T], U16, "key_words")
         nc.sync.dma_start(key_words[:].bitcast(I32), keys_words[0].bitcast(I32))
@@ -209,14 +209,16 @@ def tile_attend_slotattn_pl_kernel(tc, query, keys_words, keys_scales, fac, vals
         vals_bf3 = sb([P, I], BF16, "vals_bf3")
         turn(vals_listed3, "scores3", nc.scalar.copy, vals_bf3)
         quantise_vals(vals_bf2, sb([P, P], U32, "val_codes2"))
+        product2 = psum.tile([P, Q], F32, name="scores0")
+        multiply(product2[:], 2, slice(0, Q))
+        nc.scalar.copy(result[:, 2, :], product2[:])
+        nc.sync.dma_start(out_rows[:, 2, :], result[:, 2, :])
         quantise_vals(vals_bf3, sb([P, P], U32, "val_codes3"))
-        sums23 = [psum.tile([P, 2, HALF_Q], F32, name="sums23_%d" % half) for half in range(2)]
-        for j in (2, 3):
-            for half in (1, 0):
-                multiply(sums23[half][:, j - 2, :], j, halves[half])
         for half, copy in ((1, nc.scalar.copy), (0, nc.vector.tensor_copy)):
-            copy(result[:, 2:, halves[half]], sums23[half][:])
-        nc.sync.dma_start(out_rows[:, 2:, :], result[:, 2:, :])
+            product3 = psum.tile([P, HALF_Q], F32, name="product3_%d" % half)
+            multiply(product3[:], 3, halves[half])
+            copy(result[:, 3, halves[half]], product3[:])
+        nc.sync.dma_start(out_rows[:, 3, :], result[:, 3, :])
 
         plane_codes = sb([P, Q], U32, "plane_codes")
         plane_scales = sb([P, Q], U8, "plane_scales")
@@ -224,14 +226,15 @@ def tile_attend_slotattn_pl_kernel(tc, query, keys_words, keys_scales, fac, vals
         interleave(nc.vector.tensor_copy, result_bf[1][:], result[:, :, halves[1]])
         interleave(nc.scalar.copy, result_bf[0][:, :SCALAR_Q, :], result[:, :, :SCALAR_Q])
         interleave(nc.vector.tensor_copy, result_bf[0][:, SCALAR_Q:, :], result[:, :, SCALAR_Q:HALF_Q])
+        out_words = out_1[0].rearrange("p c r -> p (c r)").bitcast(I32)
         for half in (1, 0):
             nc.vector.quantize_mx(
                 out=plane_codes[:, halves[half]].bitcast(FP8X4),
                 scales=plane_scales[:, halves[half]],
                 in_=result_bf[half][:].rearrange("p q j -> p (q j)"),
             )
-        nc.sync.dma_start(out_1[0].rearrange("p c r -> p (c r)").bitcast(I32), plane_codes[:].bitcast(I32))
+            nc.sync.dma_start(out_words[:, halves[half]], plane_codes[:, halves[half]].bitcast(I32))
         out_scale_rows = out_2[0].rearrange("(quad r) q -> r quad q", r=4)
         for r in range(4):
-            engine = nc.sync if r == 3 else nc.scalar
+            engine = nc.sync if r >= 2 else nc.scalar
             engine.dma_start(out_scale_rows[r].bitcast(I32), plane_scales[r:P:32, :].bitcast(I32))

@@ -21,11 +21,11 @@ AXIS = mybir.AxisListType
 P = 128
 PACK = 4
 HALF_Q = Q // 2
-SCALAR_Q = 64
 POOL_BYTES = T * 4
 FIRST_ROW = 32
 ROW_STEP = 4
 LAST_VECTOR = 256
+SPARE = PACK * POOL_BYTES
 
 
 def tile_attend_slotattn_pl_kernel(tc, query, keys_words, keys_scales, fac, vals, offs, out_0, out_1, out_2):
@@ -38,48 +38,53 @@ def tile_attend_slotattn_pl_kernel(tc, query, keys_words, keys_scales, fac, vals
         def sb(shape, dtype, name):
             return keep.tile(shape, dtype, name=name, align_bytes=64)
 
-        def over_pool(j, at, shape, dtype, name):
-            return reuse.tile(shape, dtype, name=name, align_bytes=64, offset=j * POOL_BYTES + at)
+        def placed(at, shape, dtype, name):
+            return reuse.tile(shape, dtype, name=name, align_bytes=64, offset=at)
 
-        key_scales = over_pool(1, 0, [P, T], U8, "key_scales")
+        def copy_act(out, in_):
+            nc.scalar.activation(out=out, in_=in_, func=ACT.Copy)
+
+        def by_fours(ap, pattern):
+            return ap.rearrange(pattern, i=4)
+
+        def interleave(copy, out, rows):
+            copy(by_fours(out, "p (c i) t -> p c t i"), by_fours(rows, "p t (c i) -> p c t i"))
+
+        def quantise(codes, scales, values):
+            nc.vector.quantize_mx(out=codes.bitcast(FP8X4), scales=scales, in_=values)
+
+        key_scales = placed(1 * POOL_BYTES, [P, T], U8, "key_scales")
         nc.vector.memset(key_scales[:].bitcast(I32), 0)
         offsets = keep.tile([P, I // 16], U16, name="offsets")
         query_rows = [sb([P, 2, Q], F32, "query_rows%d" % u) for u in range(2)]
         query_pairs = query.rearrange("(p u j) q -> u p j q", u=2, j=2)
         nc.sync.dma_start(query_rows[0][:], query_pairs[0])
         nc.sync.dma_start(offsets[:], offs)
-        nc.sync.dma_start(key_scales[FIRST_ROW : FIRST_ROW + 16 * ROW_STEP : ROW_STEP, :].bitcast(I32), keys_scales[0].bitcast(I32))
-        key_words = over_pool(2, 0, [P, T], U16, "key_words")
+        nc.sync.dma_start(
+            key_scales[FIRST_ROW : FIRST_ROW + 16 * ROW_STEP : ROW_STEP, :].bitcast(I32), keys_scales[0].bitcast(I32)
+        )
+        key_words = placed(2 * POOL_BYTES, [P, T], U16, "key_words")
         nc.sync.dma_start(key_words[:].bitcast(I32), keys_words[0].bitcast(I32))
         nc.sync.dma_start(query_rows[1][:], query_pairs[1])
-        fac_rows = sb([P, PACK], F32, "fac_rows")
         vals_rows = vals.rearrange("(p j) t -> j p t", j=PACK)
         val_pool = []
 
         def load_vals(j):
-            tile = over_pool(j, 0, [P, T], F32, "val_pool%d" % j)
+            tile = placed(j * POOL_BYTES, [P, T], F32, "val_pool%d" % j)
             nc.sync.dma_start(tile[:], vals_rows[j])
             val_pool.append(tile)
 
         load_vals(0)
+        fac_rows = sb([P, PACK], F32, "fac_rows")
         nc.sync.dma_start(fac_rows[:], fac.rearrange("(p t) o -> p (t o)", t=PACK))
 
         identity = sb([P, P], F32, "identity")
         nc.vector.memset(identity[:], 0.0)
         make_identity(nc, identity[:], nomemset=True)
 
-        scales_listed = over_pool(PACK, 0, [P, I], U8, "scales_listed")
+        scales_listed = sb([P, I], U8, "scales_listed")
         scales_dealt = sb([P, I], U8, "scales_dealt")
         nc.vector.memset(scales_dealt[:].bitcast(I32), 0)
-        words_listed = over_pool(3, 0, [P, I], U16, "words_listed")
-        words_dealt = sb([P, I], U16, "words_dealt")
-
-        def deal(dealt, listed):
-            nc.vector.tensor_copy(
-                dealt[:].rearrange("p (t s) -> p t s", t=PACK),
-                listed[:].rearrange("p (s t) -> p t s", t=PACK),
-            )
-
         nc.vector.tensor_copy(
             scales_listed[:].rearrange("p (t s) -> p s t", t=PACK), key_scales[:].indirect(offsets[:])
         )
@@ -87,24 +92,24 @@ def tile_attend_slotattn_pl_kernel(tc, query, keys_words, keys_scales, fac, vals
             first = FIRST_ROW + r * ROW_STEP
             rows = scales_listed[first : first + 13 * ROW_STEP : 4 * ROW_STEP, :]
             nc.sync.dma_start(scales_dealt[r:P:32, :].bitcast(I32), rows.bitcast(I32))
+        words_listed = placed(3 * POOL_BYTES, [P, I], U16, "words_listed")
+        words_dealt = sb([P, I], U16, "words_dealt")
         nc.vector.tensor_copy(words_listed[:], key_words[:].indirect(offsets[:]))
-        deal(words_dealt, words_listed)
+        nc.vector.tensor_copy(
+            words_dealt[:].rearrange("p (t s) -> p t s", t=PACK),
+            words_listed[:].rearrange("p (s t) -> p t s", t=PACK),
+        )
         for j in range(1, PACK):
             load_vals(j)
 
         query_bf = sb([P, Q, PACK], BF16, "query_bf")
         for u in range(2):
-            nc.scalar.copy(
-                query_bf[:, :, 2 * u : 2 * u + 2].rearrange("p (c i) j -> p c j i", i=4),
-                query_rows[u][:].rearrange("p j (c i) -> p c j i", i=4),
-            )
+            interleave(nc.scalar.copy, query_bf[:, :, 2 * u : 2 * u + 2], query_rows[u][:])
         query_codes = sb([P, Q], U32, "query_codes")
         query_scales = sb([P, Q], U8, "query_scales")
-        nc.vector.quantize_mx(
-            out=query_codes[:].bitcast(FP8X4), scales=query_scales[:], in_=query_bf[:].rearrange("p q j -> p (q j)")
-        )
+        quantise(query_codes[:], query_scales[:], query_bf[:].rearrange("p q j -> p (q j)"))
 
-        scores = [psum.tile([P, Q], F32, name="scores%d" % t) for t in range(PACK)]
+        scores = [psum.tile([P, Q], F32, name="bank%d" % t) for t in range(PACK)]
         for t in range(PACK):
             cols = slice(t * P, (t + 1) * P)
             nc.tensor.matmul_mx(
@@ -117,123 +122,123 @@ def tile_attend_slotattn_pl_kernel(tc, query, keys_words, keys_scales, fac, vals
                 stop=True,
             )
 
-        copy_act = lambda out, in_: nc.scalar.activation(out=out, in_=in_, func=ACT.Copy)
-
-        def gather(j, vals_listed, pieces):
+        def gather(j, listed, pieces):
             for copy, first, last in pieces:
-                copy(vals_listed[:, first:last], val_pool[j][:].indirect(offsets[:, first // 16 : last // 16]))
+                copy(listed[:, first:last], val_pool[j][:].indirect(offsets[:, first // 16 : last // 16]))
 
-        def turn(vals_listed, bank, copy, vals_bf):
+        def turn(listed, bank, copy, turned_bf):
             turned = psum.tile([P, 2, P], F32, name=bank)
-            pairs = vals_listed[:].bitcast(F32)
+            pairs = listed[:].bitcast(F32)
             for u in range(2):
                 nc.tensor.transpose(turned[:, u, :], pairs[:, u : 2 * P : 2], identity[:])
-            copy(vals_bf[:].bitcast(F32).rearrange("p (e u) -> p e u", u=2), turned[:].rearrange("p u e -> p e u"))
-
-        def quantise_vals(vals_bf, val_codes):
-            val_scales = sb([P, P], U8, "val_scales%d" % len(val_mx))
-            nc.vector.quantize_mx(out=val_codes[:].bitcast(FP8X4), scales=val_scales[:], in_=vals_bf[:])
-            val_mx.append((val_codes, val_scales))
+            copy(turned_bf[:].bitcast(F32).rearrange("p (e u) -> p e u", u=2), turned[:].rearrange("p u e -> p e u"))
 
         val_mx = []
-        vals_bf = [sb([P, I], BF16, "vals_bf%d" % j) for j in range(2)]
-        vals_listed0 = sb([P, I], BF16, "vals_listed0")
-        gather(0, vals_listed0, [(copy_act, 0, I)])
+
+        def quantise_vals(turned_bf):
+            j = len(val_mx)
+            codes = sb([P, P], U32, "val_codes%d" % j)
+            scales = sb([P, P], U8, "val_scales%d" % j)
+            quantise(codes[:], scales[:], turned_bf[:])
+            val_mx.append((codes, scales))
+
+        listed0 = sb([P, I], BF16, "listed0")
+        gather(0, listed0, [(copy_act, 0, I)])
 
         probs = sb([P, PACK, Q], F32, "probs")
         sums = sb([P, PACK], F32, "sums")
         for t in range(PACK):
-            neg_max = over_pool(PACK, 8192 + 1024 * t, [P, 1], F32, "neg_max%d" % t)
+            neg_max = placed(SPARE + 1024 * t, [P, 1], F32, "neg_max%d" % t)
             nc.vector.tensor_reduce(out=neg_max[:], in_=scores[t][:], axis=AXIS.X, op=ALU.max, negate=True)
             nc.scalar.activation(
                 out=probs[:, t, :], in_=scores[t][:], func=ACT.Exp,
                 bias=neg_max[:], scale=1.0, accum_out=sums[:, t : t + 1],
             )
 
-        turn(vals_listed0, "scores0", nc.vector.tensor_copy, vals_bf[0])
-        vals_listed1 = over_pool(PACK, 8192 + 2048, [P, I], BF16, "vals_listed1")
-        gather(1, vals_listed1, [(copy_act, 0, I)])
+        turned0 = sb([P, I], BF16, "turned0")
+        turn(listed0, "bank0", nc.vector.tensor_copy, turned0)
+        listed1 = placed(SPARE + 2048, [P, I], BF16, "listed1")
+        gather(1, listed1, [(copy_act, 0, I)])
 
         inverse = sb([P, PACK], F32, "inverse")
         nc.vector.reciprocal(inverse[:], sums[:])
-        quantise_vals(vals_bf[0], sb([P, P], U32, "val_codes0"))
+        quantise_vals(turned0)
         share = sb([P, PACK], F32, "share")
         nc.vector.tensor_tensor(share[:], inverse[:], fac_rows[:], ALU.mult)
         weight_bf = sb([P, Q, PACK], BF16, "weight_bf")
         nc.vector.tensor_tensor(
-            weight_bf[:].rearrange("p (c i) t -> p c t i", i=4),
-            probs[:].rearrange("p t (c i) -> p c t i", i=4),
+            by_fours(weight_bf[:], "p (c i) t -> p c t i"),
+            by_fours(probs[:], "p t (c i) -> p c t i"),
             share[:].unsqueeze(1).unsqueeze(3).to_broadcast([P, Q // 4, PACK, 4]),
             ALU.mult,
         )
-        turn(vals_listed1, "scores1", nc.vector.tensor_copy, vals_bf[1])
+        turned1 = sb([P, I], BF16, "turned1")
+        turn(listed1, "bank1", nc.vector.tensor_copy, turned1)
         weight_codes = sb([P, Q], U32, "weight_codes")
         weight_scales = sb([P, Q], U8, "weight_scales")
-        nc.vector.quantize_mx(
-            out=weight_codes[:].bitcast(FP8X4), scales=weight_scales[:], in_=weight_bf[:].rearrange("p q t -> p (q t)")
-        )
-        quantise_vals(vals_bf[1], sb([P, P], U32, "val_codes1"))
+        quantise(weight_codes[:], weight_scales[:], weight_bf[:].rearrange("p q t -> p (q t)"))
+        quantise_vals(turned1)
 
-        vals_listed2 = sb([P, I], BF16, "vals_listed2")
-        gather(2, vals_listed2, [(copy_act, 0, I)])
-        halves = [slice(half * HALF_Q, (half + 1) * HALF_Q) for half in range(2)]
-
-        def interleave(copy, out, rows):
-            copy(out.rearrange("p (c i) t -> p c t i", i=4), rows.rearrange("p t (c i) -> p c t i", i=4))
-
+        listed2 = sb([P, I], BF16, "listed2")
+        gather(2, listed2, [(copy_act, 0, I)])
+        direct, copied = slice(0, HALF_Q), slice(HALF_Q, Q)
         out_rows = out_0.rearrange("(p j) q -> p j q", j=PACK)
 
         def multiply(out, j, cols):
-            val_codes, val_scales = val_mx[j]
+            codes, scales = val_mx[j]
             nc.tensor.matmul_mx(
                 out=out,
-                lhsT=val_codes[:].bitcast(FP8X4),
-                lhsT_scale=val_scales[:],
+                lhsT=codes[:].bitcast(FP8X4),
+                lhsT_scale=scales[:],
                 rhs=weight_codes[:, cols].bitcast(FP8X4),
                 rhs_scale=weight_scales[:, cols],
                 start=True,
                 stop=True,
             )
 
-        vals_listed3 = sb([P, I], BF16, "vals_listed3")
-        gather(3, vals_listed3, [(nc.vector.tensor_copy, 0, LAST_VECTOR), (copy_act, LAST_VECTOR, I)])
-        result = over_pool(3, 0, [P, PACK, Q], F32, "result")
-        products = [psum.tile([P, Q], F32, name="sums%d" % j) for j in range(2)]
+        listed3 = sb([P, I], BF16, "listed3")
+        gather(3, listed3, [(nc.vector.tensor_copy, 0, LAST_VECTOR), (copy_act, LAST_VECTOR, I)])
+        result = placed(3 * POOL_BYTES, [P, PACK, Q], F32, "result")
+        products = [psum.tile([P, Q], F32, name="bank%d" % (4 + j)) for j in range(2)]
         for j in range(2):
             multiply(products[j][:], j, slice(0, Q))
         nc.scalar.copy(result[:, 0, :], products[0][:])
-        vals_bf2 = over_pool(3, 4096, [P, I], BF16, "vals_bf2")
-        turn(vals_listed2, "scores2", nc.vector.tensor_copy, vals_bf2)
+        turned2 = placed(3 * POOL_BYTES + 4096, [P, I], BF16, "turned2")
+        turn(listed2, "bank2", nc.vector.tensor_copy, turned2)
         nc.vector.tensor_copy(result[:, 1, :], products[1][:])
         nc.sync.dma_start(out_rows[:, :2, :], result[:, :2, :])
-        vals_bf3 = sb([P, I], BF16, "vals_bf3")
-        turn(vals_listed3, "scores3", nc.scalar.copy, vals_bf3)
-        quantise_vals(vals_bf2, sb([P, P], U32, "val_codes2"))
-        product2 = psum.tile([P, Q], F32, name="scores0")
+        turned3 = placed(SPARE + 4096 + 512, [P, I], BF16, "turned3")
+        turn(listed3, "bank3", nc.scalar.copy, turned3)
+        quantise_vals(turned2)
+        product2 = psum.tile([P, Q], F32, name="bank0")
         multiply(product2[:], 2, slice(0, Q))
+        late = psum.tile([P, 2, HALF_Q], F32, name="bank6")
+        multiply(late[:, 0, :], 2, direct)
         nc.scalar.copy(result[:, 2, :], product2[:])
         nc.sync.dma_start(out_rows[:, 2, :], result[:, 2, :])
-        quantise_vals(vals_bf3, sb([P, P], U32, "val_codes3"))
-        for half, copy in ((1, nc.scalar.copy), (0, nc.vector.tensor_copy)):
-            product3 = psum.tile([P, HALF_Q], F32, name="product3_%d" % half)
-            multiply(product3[:], 3, halves[half])
-            copy(result[:, 3, halves[half]], product3[:])
+        quantise_vals(turned3)
+
+        result_bf = [placed(SPARE + 4096 + 1024 * h, [P, HALF_Q, PACK], BF16, "result_bf%d" % h) for h in range(2)]
+        for h, cols in enumerate((direct, copied)):
+            interleave(nc.vector.tensor_copy, result_bf[h][:, :, :2], result[:, :2, cols])
+
+        product3_copied = psum.tile([P, HALF_Q], F32, name="bank7")
+        multiply(product3_copied[:], 3, copied)
+        multiply(late[:, 1, :], 3, direct)
+        product3_direct = psum.tile([P, HALF_Q], F32, name="bank1")
+        multiply(product3_direct[:], 3, direct)
+        nc.scalar.copy(result[:, 3, copied], product3_copied[:])
+        nc.scalar.copy(result[:, 3, direct], product3_direct[:])
         nc.sync.dma_start(out_rows[:, 3, :], result[:, 3, :])
 
         plane_codes = sb([P, Q], U32, "plane_codes")
         plane_scales = sb([P, Q], U8, "plane_scales")
-        result_bf = [sb([P, HALF_Q, PACK], BF16, "result_bf%d" % half) for half in range(2)]
-        interleave(nc.vector.tensor_copy, result_bf[1][:], result[:, :, halves[1]])
-        interleave(nc.scalar.copy, result_bf[0][:, :SCALAR_Q, :], result[:, :, :SCALAR_Q])
-        interleave(nc.vector.tensor_copy, result_bf[0][:, SCALAR_Q:, :], result[:, :, SCALAR_Q:HALF_Q])
+        nc.vector.tensor_copy(result_bf[0][:, :, 2:], late[:].rearrange("p j q -> p q j"))
+        interleave(nc.vector.tensor_copy, result_bf[1][:, :, 2:], result[:, 2:, copied])
         out_words = out_1[0].rearrange("p c r -> p (c r)").bitcast(I32)
-        for half in (1, 0):
-            nc.vector.quantize_mx(
-                out=plane_codes[:, halves[half]].bitcast(FP8X4),
-                scales=plane_scales[:, halves[half]],
-                in_=result_bf[half][:].rearrange("p q j -> p (q j)"),
-            )
-            nc.sync.dma_start(out_words[:, halves[half]], plane_codes[:, halves[half]].bitcast(I32))
+        for h, cols in enumerate((direct, copied)):
+            quantise(plane_codes[:, cols], plane_scales[:, cols], result_bf[h][:].rearrange("p q j -> p (q j)"))
+            nc.sync.dma_start(out_words[:, cols], plane_codes[:, cols].bitcast(I32))
         out_scale_rows = out_2[0].rearrange("(quad r) q -> r quad q", r=4)
         for r in range(4):
             engine = nc.sync if r >= 2 else nc.scalar

@@ -126,20 +126,25 @@ def tile_attend_slotattn_pl_kernel(tc, query, keys_words, keys_scales, fac, vals
             for copy, first, last in pieces:
                 copy(listed[:, first:last], val_pool[j][:].indirect(offsets[:, first // 16 : last // 16]))
 
-        def turn(listed, bank, copy, turned_bf):
+        def turn(listed, bank, copy, turned_bf, parts=1):
             turned = psum.tile([P, 2, P], F32, name=bank)
             pairs = listed[:].bitcast(F32)
             for u in range(2):
                 nc.tensor.transpose(turned[:, u, :], pairs[:, u : 2 * P : 2], identity[:])
-            copy(turned_bf[:].bitcast(F32).rearrange("p (e u) -> p e u", u=2), turned[:].rearrange("p u e -> p e u"))
+            words = turned_bf[:].bitcast(F32).rearrange("p (e u) -> p e u", u=2)
+            for part in range(parts):
+                cols = slice(part * P // parts, (part + 1) * P // parts)
+                copy(words[:, cols, :], turned[:, :, cols].rearrange("p u e -> p e u"))
 
         val_mx = []
 
-        def quantise_vals(turned_bf):
+        def quantise_vals(turned_bf, parts=1):
             j = len(val_mx)
             codes = sb([P, P], U32, "val_codes%d" % j)
             scales = sb([P, P], U8, "val_scales%d" % j)
-            quantise(codes[:], scales[:], turned_bf[:])
+            for part in range(parts):
+                first, last = part * P // parts, (part + 1) * P // parts
+                quantise(codes[:, first:last], scales[:, first:last], turned_bf[:, PACK * first : PACK * last])
             val_mx.append((codes, scales))
 
         listed0 = sb([P, I], BF16, "listed0")
@@ -208,7 +213,7 @@ def tile_attend_slotattn_pl_kernel(tc, query, keys_words, keys_scales, fac, vals
         nc.vector.tensor_copy(result[:, 1, :], products[1][:])
         nc.sync.dma_start(out_rows[:, :2, :], result[:, :2, :])
         turned3 = placed(SPARE + 4096 + 512, [P, I], BF16, "turned3")
-        turn(listed3, "bank3", nc.scalar.copy, turned3)
+        turn(listed3, "bank3", nc.scalar.copy, turned3, 2)
         quantise_vals(turned2)
         product2 = psum.tile([P, Q], F32, name="bank0")
         multiply(product2[:], 2, slice(0, Q))
@@ -216,7 +221,7 @@ def tile_attend_slotattn_pl_kernel(tc, query, keys_words, keys_scales, fac, vals
         multiply(late[:, 0, :], 2, direct)
         nc.scalar.copy(result[:, 2, :], product2[:])
         nc.sync.dma_start(out_rows[:, 2, :], result[:, 2, :])
-        quantise_vals(turned3)
+        quantise_vals(turned3, 2)
 
         result_bf = [placed(SPARE + 4096 + 1024 * h, [P, HALF_Q, PACK], BF16, "result_bf%d" % h) for h in range(2)]
         for h, cols in enumerate((direct, copied)):

@@ -209,12 +209,12 @@ def tile_attend_slotattn_pl_kernel(tc, query, keys_words, keys_scales, fac, vals
             multiply(products[j][:], j, slice(0, Q))
         nc.scalar.copy(result[:, 0, :], products[0][:])
         turned2 = placed(3 * POOL_BYTES + 4096, [P, I], BF16, "turned2")
-        turn(listed2, "bank2", nc.vector.tensor_copy, turned2)
-        nc.vector.tensor_copy(result[:, 1, :], products[1][:])
+        turn(listed2, "bank2", nc.vector.tensor_copy, turned2, 2)
+        nc.scalar.copy(result[:, 1, :], products[1][:])
         nc.sync.dma_start(out_rows[:, :2, :], result[:, :2, :])
         turned3 = placed(SPARE + 4096 + 512, [P, I], BF16, "turned3")
         turn(listed3, "bank3", nc.scalar.copy, turned3, 2)
-        quantise_vals(turned2)
+        quantise_vals(turned2, 2)
         product2 = psum.tile([P, Q], F32, name="bank0")
         multiply(product2[:], 2, slice(0, Q))
         late = psum.tile([P, 2, HALF_Q], F32, name="bank6")

@@ -74,13 +74,16 @@ def tile_attend_slotattn_pl_kernel(tc, query, keys_words, keys_scales, fac, vals
             nc.sync.dma_start(tile[:], vals_rows[j])
             val_pool.append(tile)
 
-        load_vals(0)
-        fac_rows = sb([P, PACK], F32, "fac_rows")
-        nc.sync.dma_start(fac_rows[:], fac.rearrange("(p t) o -> p (t o)", t=PACK))
-
         identity = sb([P, P], F32, "identity")
         nc.vector.memset(identity[:], 0.0)
         make_identity(nc, identity[:], nomemset=True)
+        fac_row = sb([P, I], F32, "fac_row")
+        nc.vector.memset(fac_row[:], 0.0)
+        nc.sync.dma_start(fac_row[0:1, :], fac.rearrange("i o -> o i"))
+        load_vals(0)
+        fac_turned = psum.tile([P, PACK, P], F32, name="bank6")
+        for t in range(PACK):
+            nc.tensor.transpose(fac_turned[:, t, :], fac_row[:, t:I:PACK], identity[:])
 
         scales_listed = sb([P, I], U8, "scales_listed")
         scales_dealt = sb([P, I], U8, "scales_dealt")
@@ -169,7 +172,7 @@ def tile_attend_slotattn_pl_kernel(tc, query, keys_words, keys_scales, fac, vals
         nc.vector.reciprocal(inverse[:], sums[:])
         quantise_vals(turned0)
         share = sb([P, PACK], F32, "share")
-        nc.vector.tensor_tensor(share[:], inverse[:], fac_rows[:], ALU.mult)
+        nc.vector.tensor_tensor(share[:], inverse[:], fac_turned[:, :, 0], ALU.mult)
         weight_bf = sb([P, Q, PACK], BF16, "weight_bf")
         nc.vector.tensor_tensor(
             by_fours(weight_bf[:], "p (c i) t -> p c t i"),
@@ -208,10 +211,11 @@ def tile_attend_slotattn_pl_kernel(tc, query, keys_words, keys_scales, fac, vals
         for j in range(2):
             multiply(products[j][:], j, slice(0, Q))
         nc.scalar.copy(result[:, 0, :], products[0][:])
+        nc.sync.dma_start(out_rows[:, 0, :], result[:, 0, :])
         turned2 = placed(3 * POOL_BYTES + 4096, [P, I], BF16, "turned2")
         turn(listed2, "bank2", nc.vector.tensor_copy, turned2, 2)
         nc.scalar.copy(result[:, 1, :], products[1][:])
-        nc.sync.dma_start(out_rows[:, :2, :], result[:, :2, :])
+        nc.sync.dma_start(out_rows[:, 1, :], result[:, 1, :])
         turned3 = placed(SPARE + 4096 + 512, [P, I], BF16, "turned3")
         turn(listed3, "bank3", nc.scalar.copy, turned3, 2)
         quantise_vals(turned2, 2)

@@ -189,7 +189,7 @@ def tile_attend_slotattn_pl_kernel(tc, query, keys_words, keys_scales, fac, vals
 
         listed2 = sb([P, I], BF16, "listed2")
         gather(2, listed2, [(copy_act, 0, I)])
-        direct, copied = slice(0, HALF_Q), slice(HALF_Q, Q)
+        copied, direct = slice(0, HALF_Q), slice(HALF_Q, Q)
         out_rows = out_0.rearrange("(p j) q -> p j q", j=PACK)
 
         def multiply(out, j, cols):
@@ -224,7 +224,6 @@ def tile_attend_slotattn_pl_kernel(tc, query, keys_words, keys_scales, fac, vals
         late = psum.tile([P, 2, HALF_Q], F32, name="bank6")
         multiply(late[:, 0, :], 2, direct)
         nc.scalar.copy(result[:, 2, :], product2[:])
-        nc.sync.dma_start(out_rows[:, 2, :], result[:, 2, :])
         quantise_vals(turned3, 2)
 
         result_bf = [placed(SPARE + 4096 + 1024 * h, [P, HALF_Q, PACK], BF16, "result_bf%d" % h) for h in range(2)]
@@ -236,9 +235,12 @@ def tile_attend_slotattn_pl_kernel(tc, query, keys_words, keys_scales, fac, vals
         multiply(late[:, 1, :], 3, direct)
         product3_direct = psum.tile([P, HALF_Q], F32, name="bank1")
         multiply(product3_direct[:], 3, direct)
+        flat = "p j q -> p (j q)"
         nc.scalar.copy(result[:, 3, copied], product3_copied[:])
+        early = slice(2 * Q, 3 * Q + HALF_Q)
+        nc.sync.dma_start(out_rows.rearrange(flat)[:, early], result[:].rearrange(flat)[:, early])
         nc.scalar.copy(result[:, 3, direct], product3_direct[:])
-        nc.sync.dma_start(out_rows[:, 3, :], result[:, 3, :])
+        nc.sync.dma_start(out_rows[:, 3, direct], result[:, 3, direct])
 
         plane_codes = sb([P, Q], U32, "plane_codes")
         plane_scales = sb([P, Q], U8, "plane_scales")

@@ -189,7 +189,7 @@ def tile_attend_slotattn_pl_kernel(tc, query, keys_words, keys_scales, fac, vals
 
         listed2 = sb([P, I], BF16, "listed2")
         gather(2, listed2, [(copy_act, 0, I)])
-        copied, direct = slice(0, HALF_Q), slice(HALF_Q, Q)
+        scalar_q, vector_q = slice(0, HALF_Q), slice(HALF_Q, Q)
         out_rows = out_0.rearrange("(p j) q -> p j q", j=PACK)
 
         def multiply(out, j, cols):
@@ -219,35 +219,35 @@ def tile_attend_slotattn_pl_kernel(tc, query, keys_words, keys_scales, fac, vals
         turned3 = placed(SPARE + 4096 + 512, [P, I], BF16, "turned3")
         turn(listed3, "bank3", nc.scalar.copy, turned3, 2)
         quantise_vals(turned2, 2)
-        product2 = psum.tile([P, Q], F32, name="bank0")
-        multiply(product2[:], 2, slice(0, Q))
-        late = psum.tile([P, 2, HALF_Q], F32, name="bank6")
-        multiply(late[:, 0, :], 2, direct)
-        nc.scalar.copy(result[:, 2, :], product2[:])
+        late_scalar = psum.tile([P, 2, HALF_Q], F32, name="bank7")
+        late_vector = psum.tile([P, 2, HALF_Q], F32, name="bank6")
+        multiply(late_scalar[:, 0, :], 2, scalar_q)
+        multiply(late_vector[:, 0, :], 2, vector_q)
+        nc.scalar.copy(result[:, 2, scalar_q], late_scalar[:, 0, :])
+        nc.scalar.copy(result[:, 2, vector_q], late_vector[:, 0, :])
         quantise_vals(turned3, 2)
 
         result_bf = [placed(SPARE + 4096 + 1024 * h, [P, HALF_Q, PACK], BF16, "result_bf%d" % h) for h in range(2)]
-        for h, cols in enumerate((direct, copied)):
+        for h, cols in enumerate((scalar_q, vector_q)):
             interleave(nc.vector.tensor_copy, result_bf[h][:, :, :2], result[:, :2, cols])
 
-        product3_copied = psum.tile([P, HALF_Q], F32, name="bank7")
-        multiply(product3_copied[:], 3, copied)
-        multiply(late[:, 1, :], 3, direct)
-        product3_direct = psum.tile([P, HALF_Q], F32, name="bank1")
-        multiply(product3_direct[:], 3, direct)
+        multiply(late_scalar[:, 1, :], 3, scalar_q)
+        multiply(late_vector[:, 1, :], 3, vector_q)
+        again = psum.tile([P, HALF_Q], F32, name="bank1")
+        multiply(again[:], 3, vector_q)
         flat = "p j q -> p (j q)"
-        nc.scalar.copy(result[:, 3, copied], product3_copied[:])
+        nc.scalar.copy(result[:, 3, scalar_q], late_scalar[:, 1, :])
         early = slice(2 * Q, 3 * Q + HALF_Q)
         nc.sync.dma_start(out_rows.rearrange(flat)[:, early], result[:].rearrange(flat)[:, early])
-        nc.scalar.copy(result[:, 3, direct], product3_direct[:])
-        nc.sync.dma_start(out_rows[:, 3, direct], result[:, 3, direct])
+        nc.scalar.copy(result_bf[0][:, :, 2:], late_scalar[:].rearrange("p j q -> p q j"))
+        nc.scalar.copy(result[:, 3, vector_q], again[:])
+        nc.sync.dma_start(out_rows[:, 3, vector_q], result[:, 3, vector_q])
+        nc.vector.tensor_copy(result_bf[1][:, :, 2:], late_vector[:].rearrange("p j q -> p q j"))
 
         plane_codes = sb([P, Q], U32, "plane_codes")
         plane_scales = sb([P, Q], U8, "plane_scales")
-        nc.vector.tensor_copy(result_bf[0][:, :, 2:], late[:].rearrange("p j q -> p q j"))
-        interleave(nc.vector.tensor_copy, result_bf[1][:, :, 2:], result[:, 2:, copied])
         out_words = out_1[0].rearrange("p c r -> p (c r)").bitcast(I32)
-        for h, cols in enumerate((direct, copied)):
+        for h, cols in enumerate((scalar_q, vector_q)):
             quantise(plane_codes[:, cols], plane_scales[:, cols], result_bf[h][:].rearrange("p q j -> p (q j)"))
             nc.sync.dma_start(out_words[:, cols], plane_codes[:, cols].bitcast(I32))
         out_scale_rows = out_2[0].rearrange("(quad r) q -> r quad q", r=4)

@@ -189,7 +189,7 @@ def tile_attend_slotattn_pl_kernel(tc, query, keys_words, keys_scales, fac, vals
 
         listed2 = sb([P, I], BF16, "listed2")
         gather(2, listed2, [(copy_act, 0, I)])
-        scalar_q, vector_q = slice(0, HALF_Q), slice(HALF_Q, Q)
+        vector_q, scalar_q = slice(0, HALF_Q), slice(HALF_Q, Q)
         out_rows = out_0.rearrange("(p j) q -> p j q", j=PACK)
 
         def multiply(out, j, cols):
@@ -223,33 +223,26 @@ def tile_attend_slotattn_pl_kernel(tc, query, keys_words, keys_scales, fac, vals
         late_vector = psum.tile([P, 2, HALF_Q], F32, name="bank6")
         multiply(late_scalar[:, 0, :], 2, scalar_q)
         multiply(late_vector[:, 0, :], 2, vector_q)
-        nc.scalar.copy(result[:, 2, scalar_q], late_scalar[:, 0, :])
-        nc.scalar.copy(result[:, 2, vector_q], late_vector[:, 0, :])
+        product2 = psum.tile([P, Q], F32, name="bank0")
+        multiply(product2[:], 2, slice(0, Q))
+        nc.scalar.copy(result[:, 2, :], product2[:])
+        nc.sync.dma_start(out_rows[:, 2, :], result[:, 2, :])
         quantise_vals(turned3, 2)
 
-        result_bf = [placed(SPARE + 4096 + 1024 * h, [P, HALF_Q, PACK], BF16, "result_bf%d" % h) for h in range(2)]
-        for h, cols in enumerate((scalar_q, vector_q)):
-            interleave(nc.vector.tensor_copy, result_bf[h][:, :, :2], result[:, :2, cols])
+        result_bf = placed(SPARE + 4096, [P, Q, PACK], BF16, "result_bf")
+        interleave(nc.vector.tensor_copy, result_bf[:, :, :2], result[:, :2, :])
 
-        multiply(late_scalar[:, 1, :], 3, scalar_q)
         multiply(late_vector[:, 1, :], 3, vector_q)
-        again = psum.tile([P, HALF_Q], F32, name="bank1")
-        multiply(again[:], 3, vector_q)
-        flat = "p j q -> p (j q)"
-        nc.scalar.copy(result[:, 3, scalar_q], late_scalar[:, 1, :])
-        early = slice(2 * Q, 3 * Q + HALF_Q)
-        nc.sync.dma_start(out_rows.rearrange(flat)[:, early], result[:].rearrange(flat)[:, early])
-        nc.scalar.copy(result_bf[0][:, :, 2:], late_scalar[:].rearrange("p j q -> p q j"))
-        nc.scalar.copy(result[:, 3, vector_q], again[:])
-        nc.sync.dma_start(out_rows[:, 3, vector_q], result[:, 3, vector_q])
-        nc.vector.tensor_copy(result_bf[1][:, :, 2:], late_vector[:].rearrange("p j q -> p q j"))
+        multiply(late_scalar[:, 1, :], 3, scalar_q)
+        for copy, cols, late in ((nc.vector.tensor_copy, vector_q, late_vector), (nc.scalar.copy, scalar_q, late_scalar)):
+            copy(result_bf[:, cols, 2:], late[:].rearrange("p j q -> p q j"))
+            copy(result[:, 3, cols], late[:, 1, :])
+            nc.sync.dma_start(out_rows[:, 3, cols], result[:, 3, cols])
 
         plane_codes = sb([P, Q], U32, "plane_codes")
         plane_scales = sb([P, Q], U8, "plane_scales")
-        out_words = out_1[0].rearrange("p c r -> p (c r)").bitcast(I32)
-        for h, cols in enumerate((scalar_q, vector_q)):
-            quantise(plane_codes[:, cols], plane_scales[:, cols], result_bf[h][:].rearrange("p q j -> p (q j)"))
-            nc.sync.dma_start(out_words[:, cols], plane_codes[:, cols].bitcast(I32))
+        quantise(plane_codes[:], plane_scales[:], result_bf[:].rearrange("p q j -> p (q j)"))
+        nc.sync.dma_start(out_1[0].rearrange("p c r -> p (c r)").bitcast(I32), plane_codes[:].bitcast(I32))
         out_scale_rows = out_2[0].rearrange("(quad r) q -> r quad q", r=4)
         for r in range(4):
             engine = nc.sync if r >= 2 else nc.scalar

@@ -241,7 +241,8 @@ def tile_attend_slotattn_pl_kernel(tc, query, keys_words, keys_scales, fac, vals
 
         plane_codes = sb([P, Q], U32, "plane_codes")
         plane_scales = sb([P, Q], U8, "plane_scales")
-        quantise(plane_codes[:], plane_scales[:], result_bf[:].rearrange("p q j -> p (q j)"))
+        for cols in (vector_q, scalar_q):
+            quantise(plane_codes[:, cols], plane_scales[:, cols], result_bf[:, cols, :].rearrange("p q j -> p (q j)"))
         nc.sync.dma_start(out_1[0].rearrange("p c r -> p (c r)").bitcast(I32), plane_codes[:].bitcast(I32))
         out_scale_rows = out_2[0].rearrange("(quad r) q -> r quad q", r=4)
         for r in range(4):

from contextlib import ExitStack

import concourse.mybir as mybir
from concourse.masks import make_identity

D, T, I, Q, E = 512, 2048, 512, 256, 512
FLOPS = 2 * I * D * Q + 2 * E * I * Q

F32 = mybir.dt.float32
BF16 = mybir.dt.bfloat16
I32 = mybir.dt.int32
U32 = mybir.dt.uint32
U16 = mybir.dt.uint16
U8 = mybir.dt.uint8
FP8X4 = mybir.dt.float8_e4m3fn_x4
FP4X4 = mybir.dt.float4_e2m1fn_x4
ACT = mybir.ActivationFunctionType
ALU = mybir.AluOpType
AXIS = mybir.AxisListType

P = 128
PACK = 4
HALF_Q = Q // 2
POOL_BYTES = T * 4
FIRST_ROW = 32
ROW_STEP = 4
LAST_VECTOR = 256
SPARE = PACK * POOL_BYTES


def tile_attend_slotattn_pl_kernel(tc, query, keys_words, keys_scales, fac, vals, offs, out_0, out_1, out_2):
    nc = tc.nc
    with ExitStack() as ctx:
        keep = ctx.enter_context(tc.tile_pool(name="keep", bufs=1))
        reuse = ctx.enter_context(tc.tile_pool(name="reuse", bufs=1))
        psum = ctx.enter_context(tc.psum_pool(name="psum", bufs=1))

        def sb(shape, dtype, name):
            return keep.tile(shape, dtype, name=name, align_bytes=64)

        def placed(at, shape, dtype, name):
            return reuse.tile(shape, dtype, name=name, align_bytes=64, offset=at)

        def copy_act(out, in_):
            nc.scalar.activation(out=out, in_=in_, func=ACT.Copy)

        def by_fours(ap, pattern):
            return ap.rearrange(pattern, i=4)

        def interleave(copy, out, rows):
            copy(by_fours(out, "p (c i) t -> p c t i"), by_fours(rows, "p t (c i) -> p c t i"))

        def quantise(codes, scales, values):
            nc.vector.quantize_mx(out=codes.bitcast(FP8X4), scales=scales, in_=values)

        key_scales = placed(1 * POOL_BYTES, [P, T], U8, "key_scales")
        nc.vector.memset(key_scales[:].bitcast(I32), 0)
        offsets = keep.tile([P, I // 16], U16, name="offsets")
        query_rows = [sb([P, 2, Q], F32, "query_rows%d" % u) for u in range(2)]
        query_pairs = query.rearrange("(p u j) q -> u p j q", u=2, j=2)
        nc.sync.dma_start(query_rows[0][:], query_pairs[0])
        nc.sync.dma_start(offsets[:], offs)
        nc.sync.dma_start(
            key_scales[FIRST_ROW : FIRST_ROW + 16 * ROW_STEP : ROW_STEP, :].bitcast(I32), keys_scales[0].bitcast(I32)
        )
        key_words = placed(2 * POOL_BYTES, [P, T], U16, "key_words")
        nc.sync.dma_start(key_words[:].bitcast(I32), keys_words[0].bitcast(I32))
        nc.sync.dma_start(query_rows[1][:], query_pairs[1])
        vals_rows = vals.rearrange("(p j) t -> j p t", j=PACK)
        val_pool = []

        def load_vals(j):
            tile = placed(j * POOL_BYTES, [P, T], F32, "val_pool%d" % j)
            nc.sync.dma_start(tile[:], vals_rows[j])
            val_pool.append(tile)

        identity = sb([P, P], F32, "identity")
        nc.vector.memset(identity[:], 0.0)
        make_identity(nc, identity[:], nomemset=True)
        fac_row = sb([P, I], F32, "fac_row")
        nc.vector.memset(fac_row[:], 0.0)
        nc.sync.dma_start(fac_row[0:1, :], fac.rearrange("i o -> o i"))
        load_vals(0)
        fac_turned = psum.tile([P, PACK, P], F32, name="bank6")
        for t in range(PACK):
            nc.tensor.transpose(fac_turned[:, t, :], fac_row[:, t:I:PACK], identity[:])

        scales_listed = sb([P, I], U8, "scales_listed")
        scales_dealt = sb([P, I], U8, "scales_dealt")
        nc.vector.memset(scales_dealt[:].bitcast(I32), 0)
        nc.vector.tensor_copy(
            scales_listed[:].rearrange("p (t s) -> p s t", t=PACK), key_scales[:].indirect(offsets[:])
        )
        for r in range(4):
            first = FIRST_ROW + r * ROW_STEP
            rows = scales_listed[first : first + 13 * ROW_STEP : 4 * ROW_STEP, :]
            nc.sync.dma_start(scales_dealt[r:P:32, :].bitcast(I32), rows.bitcast(I32))
        words_listed = placed(3 * POOL_BYTES, [P, I], U16, "words_listed")
        words_dealt = sb([P, I], U16, "words_dealt")
        nc.vector.tensor_copy(words_listed[:], key_words[:].indirect(offsets[:]))
        nc.vector.tensor_copy(
            words_dealt[:].rearrange("p (t s) -> p t s", t=PACK),
            words_listed[:].rearrange("p (s t) -> p t s", t=PACK),
        )
        for j in range(1, PACK):
            load_vals(j)

        query_bf = sb([P, Q, PACK], BF16, "query_bf")
        for u in range(2):
            interleave(nc.scalar.copy, query_bf[:, :, 2 * u : 2 * u + 2], query_rows[u][:])
        query_codes = sb([P, Q], U32, "query_codes")
        query_scales = sb([P, Q], U8, "query_scales")
        quantise(query_codes[:], query_scales[:], query_bf[:].rearrange("p q j -> p (q j)"))

        scores = [psum.tile([P, Q], F32, name="bank%d" % t) for t in range(PACK)]
        for t in range(PACK):
            cols = slice(t * P, (t + 1) * P)
            nc.tensor.matmul_mx(
                out=scores[t][:],
                lhsT=words_dealt[:, cols].bitcast(FP4X4),
                lhsT_scale=scales_dealt[:, cols],
                rhs=query_codes[:].bitcast(FP8X4),
                rhs_scale=query_scales[:],
                start=True,
                stop=True,
            )

        def gather(j, listed, pieces):
            for copy, first, last in pieces:
                copy(listed[:, first:last], val_pool[j][:].indirect(offsets[:, first // 16 : last // 16]))

        def turn(listed, bank, copy, turned_bf, parts=1):
            turned = psum.tile([P, 2, P], F32, name=bank)
            pairs = listed[:].bitcast(F32)
            for u in range(2):
                nc.tensor.transpose(turned[:, u, :], pairs[:, u : 2 * P : 2], identity[:])
            words = turned_bf[:].bitcast(F32).rearrange("p (e u) -> p e u", u=2)
            for part in range(parts):
                cols = slice(part * P // parts, (part + 1) * P // parts)
                copy(words[:, cols, :], turned[:, :, cols].rearrange("p u e -> p e u"))

        val_mx = []

        def quantise_vals(turned_bf, parts=1):
            j = len(val_mx)
            codes = sb([P, P], U32, "val_codes%d" % j)
            scales = sb([P, P], U8, "val_scales%d" % j)
            for part in range(parts):
                first, last = part * P // parts, (part + 1) * P // parts
                quantise(codes[:, first:last], scales[:, first:last], turned_bf[:, PACK * first : PACK * last])
            val_mx.append((codes, scales))

        listed0 = sb([P, I], BF16, "listed0")
        gather(0, listed0, [(copy_act, 0, I)])

        probs = sb([P, PACK, Q], F32, "probs")
        sums = sb([P, PACK], F32, "sums")
        for t in range(PACK):
            neg_max = placed(SPARE + 1024 * t, [P, 1], F32, "neg_max%d" % t)
            nc.vector.tensor_reduce(out=neg_max[:], in_=scores[t][:], axis=AXIS.X, op=ALU.max, negate=True)
            nc.scalar.activation(
                out=probs[:, t, :], in_=scores[t][:], func=ACT.Exp,
                bias=neg_max[:], scale=1.0, accum_out=sums[:, t : t + 1],
            )

        turned0 = sb([P, I], BF16, "turned0")
        turn(listed0, "bank0", nc.vector.tensor_copy, turned0)
        listed1 = placed(SPARE + 2048, [P, I], BF16, "listed1")
        gather(1, listed1, [(copy_act, 0, I)])

        inverse = sb([P, PACK], F32, "inverse")
        nc.vector.reciprocal(inverse[:], sums[:])
        quantise_vals(turned0)
        share = sb([P, PACK], F32, "share")
        nc.vector.tensor_tensor(share[:], inverse[:], fac_turned[:, :, 0], ALU.mult)
        weight_bf = sb([P, Q, PACK], BF16, "weight_bf")
        nc.vector.tensor_tensor(
            by_fours(weight_bf[:], "p (c i) t -> p c t i"),
            by_fours(probs[:], "p t (c i) -> p c t i"),
            share[:].unsqueeze(1).unsqueeze(3).to_broadcast([P, Q // 4, PACK, 4]),
            ALU.mult,
        )
        turned1 = sb([P, I], BF16, "turned1")
        turn(listed1, "bank1", nc.vector.tensor_copy, turned1)
        weight_codes = sb([P, Q], U32, "weight_codes")
        weight_scales = sb([P, Q], U8, "weight_scales")
        quantise(weight_codes[:], weight_scales[:], weight_bf[:].rearrange("p q t -> p (q t)"))
        quantise_vals(turned1)

        listed2 = sb([P, I], BF16, "listed2")
        gather(2, listed2, [(copy_act, 0, I)])
        vector_q, scalar_q = slice(0, HALF_Q), slice(HALF_Q, Q)
        out_rows = out_0.rearrange("(p j) q -> p j q", j=PACK)

        def multiply(out, j, cols):
            codes, scales = val_mx[j]
            nc.tensor.matmul_mx(
                out=out,
                lhsT=codes[:].bitcast(FP8X4),
                lhsT_scale=scales[:],
                rhs=weight_codes[:, cols].bitcast(FP8X4),
                rhs_scale=weight_scales[:, cols],
                start=True,
                stop=True,
            )

        listed3 = sb([P, I], BF16, "listed3")
        gather(3, listed3, [(nc.vector.tensor_copy, 0, LAST_VECTOR), (copy_act, LAST_VECTOR, I)])
        result = placed(3 * POOL_BYTES, [P, PACK, Q], F32, "result")
        products = [psum.tile([P, Q], F32, name="bank%d" % (4 + j)) for j in range(2)]
        for j in range(2):
            multiply(products[j][:], j, slice(0, Q))
        nc.scalar.copy(result[:, 0, :], products[0][:])
        nc.sync.dma_start(out_rows[:, 0, :], result[:, 0, :])
        turned2 = placed(3 * POOL_BYTES + 4096, [P, I], BF16, "turned2")
        turn(listed2, "bank2", nc.vector.tensor_copy, turned2, 2)
        nc.scalar.copy(result[:, 1, :], products[1][:])
        nc.sync.dma_start(out_rows[:, 1, :], result[:, 1, :])
        turned3 = placed(SPARE + 4096 + 512, [P, I], BF16, "turned3")
        turn(listed3, "bank3", nc.scalar.copy, turned3, 2)
        quantise_vals(turned2, 2)
        late_scalar = psum.tile([P, 2, HALF_Q], F32, name="bank7")
        late_vector = psum.tile([P, 2, HALF_Q], F32, name="bank6")
        multiply(late_scalar[:, 0, :], 2, scalar_q)
        multiply(late_vector[:, 0, :], 2, vector_q)
        product2 = psum.tile([P, Q], F32, name="bank0")
        multiply(product2[:], 2, slice(0, Q))
        nc.scalar.copy(result[:, 2, :], product2[:])
        nc.sync.dma_start(out_rows[:, 2, :], result[:, 2, :])
        quantise_vals(turned3, 2)

        result_bf = placed(SPARE + 4096, [P, Q, PACK], BF16, "result_bf")
        interleave(nc.vector.tensor_copy, result_bf[:, :, :2], result[:, :2, :])

        multiply(late_vector[:, 1, :], 3, vector_q)
        multiply(late_scalar[:, 1, :], 3, scalar_q)
        for copy, cols, late in ((nc.vector.tensor_copy, vector_q, late_vector), (nc.scalar.copy, scalar_q, late_scalar)):
            copy(result_bf[:, cols, 2:], late[:].rearrange("p j q -> p q j"))
            copy(result[:, 3, cols], late[:, 1, :])
            nc.sync.dma_start(out_rows[:, 3, cols], result[:, 3, cols])

        plane_codes = sb([P, Q], U32, "plane_codes")
        plane_scales = sb([P, Q], U8, "plane_scales")
        for cols in (vector_q, scalar_q):
            quantise(plane_codes[:, cols], plane_scales[:, cols], result_bf[:, cols, :].rearrange("p q j -> p (q j)"))
        nc.sync.dma_start(out_1[0].rearrange("p c r -> p (c r)").bitcast(I32), plane_codes[:].bitcast(I32))
        out_scale_rows = out_2[0].rearrange("(quad r) q -> r quad q", r=4)
        for r in range(4):
            engine = nc.sync if r >= 2 else nc.scalar
            engine.dma_start(out_scale_rows[r].bitcast(I32), plane_scales[r:P:32, :].bitcast(I32))
